import numpy as np
import ml_dtypes


def mxq(x, axis, fmt="e4m3"):
    dtype, down = {"e4m3": (ml_dtypes.float8_e4m3fn, 7), "e5m2": (ml_dtypes.float8_e5m2, 14)}[fmt]
    v = np.moveaxis(np.asarray(x, np.float32).astype(ml_dtypes.bfloat16).astype(np.float64), axis, -1)
    blocks = v.reshape(v.shape[:-1] + (-1, 32))
    amax = np.abs(blocks).max(-1, keepdims=True)
    byte = np.maximum(np.where(amax > 0, np.frexp(amax)[1] - 1 + 127, 0) - down, 1)
    scale = np.exp2(byte - 127.0)
    codes = (blocks / scale).astype(np.float32).astype(dtype).astype(np.float64)
    return np.moveaxis((codes * scale).reshape(v.shape), -1, axis)


WIDE = False


def mx_kscale(k):
    if not WIDE:
        return np.ones(k)
    levels = np.array([10, -10, 5, -5, 0])
    if k % 512:
        return np.exp2(np.random.permutation(np.resize(levels, k // 32))).repeat(32)
    a = np.empty((k // 512, 16))
    for p in range(k // 512):
        a[p, :8] = np.random.permutation(np.resize(levels, 8))
        for g in range(8):
            far = levels[np.abs(levels - a[p, g]) >= 10]
            a[p, g + 8] = far[np.random.randint(len(far))]
    return np.exp2(a.ravel()).repeat(32)


def f64(x):
    return np.asarray(x).astype(np.float64)


def striped(idx):
    return np.tile(np.asarray(idx).reshape(-1, 16).T, (8, 1)).astype(np.uint16)


def unstriped(offs):
    return offs[:16].T.reshape(-1).astype(np.int64)


B, N, T, D, DV, NQ = 1, 512, 1024, 512, 256, 256


def setup_inputs():
    n = np.random.standard_normal
    idx = np.random.permutation(T)[:B * N]
    s = mx_kscale(D)[:, None]
    u = np.ones(T)
    u[idx] = mx_kscale(B * N)
    r = np.random.uniform(0.5, 2.0, T)
    qidx = np.random.permutation(T)[:B * NQ]
    k = n((D, T)) / s
    v = n((DV, T)) / (u * r)
    return {
        "xq": (n((D, T)) * s * (0.60 / np.sqrt(D))).astype(np.float32),
        "kT": k.astype(np.float32),
        "vT": v.astype(np.float32),
        "vs": np.tile(u * r, (128, 1)).astype(np.float32),
        "sink": (2.0 + 3.0 * n((B, NQ, 1))).astype(np.float32),
        "offs": striped(idx),
        "qoffs": striped(qidx),
    }


def reference(xq, kT, vT, vs, sink, offs, qoffs):
    idx = unstriped(offs)
    k = f64(kT)
    v = f64(vT)
    pick = lambda x: x[:, idx].reshape(x.shape[0], B, N).transpose(1, 0, 2)
    q = f64(xq)[:, unstriped(qoffs)].reshape(D, B, NQ).transpose(1, 0, 2)
    score = mxq(q, 1, "e4m3").transpose(0, 2, 1) @ mxq(pick(k), 1, "e4m3")
    m = np.maximum(score.max(-1, keepdims=True), f64(sink))
    p = np.exp(score - m)
    total = p.sum(-1, keepdims=True) + np.exp(f64(sink) - m)
    w = p * pick(f64(vs))[:, :1, :]
    y = mxq(w, 2, "e4m3") @ mxq(pick(v).transpose(0, 2, 1), 1, "e4m3")
    y = y / total
    out = np.zeros((DV, T))
    out[:, unstriped(qoffs)] = y.transpose(2, 0, 1).reshape(-1, B * NQ)
    return out

@@ -1,0 +1,242 @@
+from contextlib import ExitStack
+
+import concourse.mybir as mybir
+from concourse.masks import make_identity
+
+D, T, N, NQ, DV = 512, 1024, 512, 256, 256
+P = 128
+FLOPS = 2 * NQ * N * D + 2 * NQ * N * DV
+
+F32 = mybir.dt.float32
+BF16 = mybir.dt.bfloat16
+U32 = mybir.dt.uint32
+U16 = mybir.dt.uint16
+U8 = mybir.dt.uint8
+FP8X4 = mybir.dt.float8_e4m3fn_x4
+
+COPY = mybir.ActivationFunctionType.Copy
+EXP = mybir.ActivationFunctionType.Exp
+MULT = mybir.AluOpType.mult
+MIN = mybir.AluOpType.min
+
+SCALAR_TOKENS = (384, 256)
+
+
+def tile_attend_x_router_sink_kernel(tc, xq, kT, vT, vs, sink, offs, qoffs, out):
+    nc = tc.nc
+    with ExitStack() as ctx:
+        keep = ctx.enter_context(tc.tile_pool(name="keep", bufs=1))
+        psum = ctx.enter_context(tc.psum_pool(name="psum", bufs=2))
+        tiles = [slice(c * P, (c + 1) * P) for c in range(2)]
+
+        offs_t = keep.tile([P, N // 16], U16, name="offs_t")
+        qoffs_t = keep.tile([P, NQ // 16], U16, name="qoffs_t")
+        k_raw = [keep.tile([P, 2, T], F32, name=f"k_raw{u}", tag=f"k_raw{u}", align_bytes=64) for u in range(2)]
+        v_raw = [keep.tile([P, T], F32, name=f"v_raw{h}") for h in range(2)]
+        q_raw = [keep.tile([P, T], F32, name=f"q_raw{j}") for j in range(4)]
+        vs_raw = keep.tile([P, T], F32, name="vs_raw")
+        k_rows = kT.rearrange("(p j) n -> p j n", j=4)
+        q_rows = xq.rearrange("(p j) n -> p j n", j=4)
+        nc.sync.dma_start(out=k_raw[0][:], in_=k_rows[:, 0:2, :])
+        nc.sync.dma_start(offs_t[:], offs)
+        nc.sync.dma_start(out=v_raw[0][:], in_=vT[tiles[0], :])
+        nc.sync.dma_start(out=k_raw[1][:], in_=k_rows[:, 2:4, :])
+        nc.sync.dma_start(qoffs_t[:], qoffs)
+        for j in range(4):
+            nc.sync.dma_start(out=q_raw[j][:], in_=q_rows[:, j, :])
+        nc.sync.dma_start(out=vs_raw[:], in_=vs)
+        nc.sync.dma_start(out=v_raw[1][:], in_=vT[tiles[1], :])
+
+        sink_row = keep.tile([P, NQ], F32, name="sink_row")
+        nc.vector.memset(sink_row[:], 0.0)
+        nc.scalar.dma_start(out=sink_row[0:1, :], in_=sink.rearrange("b q o -> b (q o)"))
+        ident = keep.tile([P, P], F32, name="ident")
+        make_identity(nc, ident[:])
+        ident_b = keep.tile([P, P], BF16, name="ident_b")
+        make_identity(nc, ident_b[:])
+        placed = [keep.tile([P, T], F32, name=f"placed{h}") for h in range(2)]
+        for h in range(2):
+            nc.gpsimd.memset(placed[h][:], 0.0)
+        table = keep.tile([P, 1], F32, name="table")
+        nc.scalar.activation(out=table[:], in_=ident[:, 0:1], func=EXP)
+
+        def turn_values(v_g):
+            v_ps = psum.tile([P, 4, P], BF16, name="v_ps", tag="turn", bufs=3)
+            for t in range(4):
+                nc.tensor.transpose(v_ps[:, t, :], v_g[:, t * P : (t + 1) * P], ident_b[:])
+            return v_ps
+
+        def interleave_values(h, v_ps):
+            v_s = keep.tile([P, P, 4], BF16, name=f"v_s{h}", align_bytes=64)
+            nc.scalar.copy(out=v_s[:], in_=v_ps[:].rearrange("s t e -> s e t"))
+            return v_s
+
+        v_codes, v_scales = [], []
+
+        def quantise_values(h, v_s):
+            codes = keep.tile([P, P], U32, name=f"v_codes{h}", tag=("flipped0", "v_codes1")[h], align_bytes=64)
+            scales = keep.tile([P, P], U8, name=f"v_scales{h}", align_bytes=64)
+            nc.vector.quantize_mx(out=codes[:].bitcast(FP8X4), scales=scales[:], in_=v_s[:].rearrange("s e t -> s (e t)"))
+            v_codes.append(codes)
+            v_scales.append(scales)
+
+        k_g = keep.tile([P, N * 4], BF16, name="k_g", align_bytes=64)
+        k_words = k_g[:].bitcast(U32).rearrange("p (t s u) -> p s t u", t=4, u=2)
+
+        def gather_keys(u):
+            k_pair = keep.tile([P, T, 2], BF16, name=f"k_pair{u}", tag="step", align_bytes=64)
+            raw = k_raw[u][:].rearrange("p e n -> p n e")
+            split = SCALAR_TOKENS[u]
+            nc.scalar.activation(out=k_pair[:, :split, :], in_=raw[:, :split, :], func=COPY)
+            nc.vector.tensor_copy(out=k_pair[:, split:, :], in_=raw[:, split:, :])
+            window = k_pair[:].rearrange("p n e -> p (n e)").bitcast(U32)
+            nc.vector.tensor_copy(k_words[:, :, :, u], window.indirect(offs_t[:]))
+
+        gather_keys(0)
+        v_cast = keep.tile([P, T], BF16, name="v_cast")
+        nc.scalar.activation(out=v_cast[:], in_=v_raw[0][:], func=COPY)
+        v_g0 = keep.tile([P, N], BF16, name="v_g0")
+        nc.scalar.activation(
+            out=v_g0[:].rearrange("p (t s) -> p s t", t=4), in_=v_cast[:].indirect(offs_t[:]), func=COPY
+        )
+        v_ps0 = turn_values(v_g0)
+        gather_keys(1)
+
+        q_cast = keep.tile([P, 2, T], BF16, name="q_cast", tag="k_raw1", align_bytes=64)
+        for j in range(2):
+            nc.scalar.activation(out=q_cast[:, j, :], in_=q_raw[j][:], func=COPY)
+        q_g = keep.tile([P, NQ, 4], BF16, name="q_g", tag="step", align_bytes=64)
+        for j in range(2):
+            nc.scalar.activation(out=q_g[:, :, j], in_=q_cast[:, j, :].indirect(qoffs_t[:]), func=COPY)
+        k_codes = keep.tile([P, N], U32, name="k_codes", align_bytes=64)
+        k_scales = keep.tile([P, N], U8, name="k_scales", align_bytes=64)
+        nc.vector.quantize_mx(out=k_codes[:].bitcast(FP8X4), scales=k_scales[:], in_=k_g[:])
+        nc.vector.tensor_copy(q_g[:, :, 2], q_raw[2][:].indirect(qoffs_t[:]))
+        v_s0 = interleave_values(0, v_ps0)
+        for c in range(2):
+            nc.vector.tensor_copy(q_g[:, tiles[c], 3], q_raw[3][:].indirect(qoffs_t[:, c * 8 : (c + 1) * 8]))
+        q_codes = keep.tile([P, NQ], U32, name="q_codes", align_bytes=64)
+        q_scales = keep.tile([P, NQ], U8, name="q_scales", align_bytes=64)
+        for cols in tiles:
+            nc.vector.quantize_mx(
+                out=q_codes[:, cols].bitcast(FP8X4), scales=q_scales[:, cols], in_=q_g[:, cols, :].rearrange("p q j -> p (q j)")
+            )
+
+        sink_ps = psum.tile([P, 2, P], F32, name="sink_ps", tag="y")
+        for c in range(2):
+            nc.tensor.transpose(sink_ps[:, c, :], sink_row[:, tiles[c]], ident[:])
+        sink_n = keep.tile([P, 2], F32, name="sink_n", tag="k_raw1", align_bytes=64)
+        nc.scalar.activation(out=sink_n[:], in_=sink_ps[:, :, 0], func=COPY, scale=-1.0)
+
+        scores = []
+        for cols in tiles:
+            score = psum.tile([P, N], F32, name="score", tag="score")
+            nc.tensor.matmul_mx(
+                out=score[:],
+                lhsT=q_codes[:, cols].bitcast(FP8X4),
+                lhsT_scale=q_scales[:, cols],
+                rhs=k_codes[:].bitcast(FP8X4),
+                rhs_scale=k_scales[:],
+                start=True,
+                stop=True,
+            )
+            scores.append(score)
+
+        vs_g = keep.tile([P, N], F32, name="vs_g", tag="step", align_bytes=64)
+        nc.vector.tensor_copy(vs_g[:], vs_raw[:].indirect(offs_t[:]))
+        vs_ps = psum.tile([P, 4, P], F32, name="vs_ps", tag="turn", bufs=3)
+        for t in range(4):
+            nc.tensor.transpose(vs_ps[:, t, :], vs_g[:, t::4], ident[:])
+
+        neg_max = []
+        for c in range(2):
+            least = keep.tile([P, 1], F32, name=f"neg_max{c}")
+            flipped = keep.tile([P, N], F32, name=f"flipped{c}", tag=f"flipped{c}", align_bytes=64)
+            nc.vector.tensor_scalar(
+                out=flipped[:],
+                in0=scores[c][:],
+                scalar1=-1.0,
+                scalar2=sink_n[:, c : c + 1],
+                op0=MULT,
+                op1=MIN,
+                accum_out=least[:],
+            )
+            neg_max.append(least)
+        terms = keep.tile([P, 2, 3], F32, name="terms")
+        p_banks = []
+        for c in range(2):
+            p = keep.tile([P, N], F32, name=f"p{c}")
+            p_ps = psum.tile([P, 4, P], F32, name="p_ps", tag="turn", bufs=3)
+            for half in range(2):
+                cols = slice(half * 2 * P, (half + 1) * 2 * P)
+                nc.scalar.activation(
+                    out=p[:, cols],
+                    in_=scores[c][:, cols],
+                    func=EXP,
+                    bias=neg_max[c][:],
+                    scale=1.0,
+                    accum_out=terms[:, c, half : half + 1],
+                )
+                for t in (2 * half, 2 * half + 1):
+                    nc.tensor.transpose(p_ps[:, t, :], p[:, t * P : (t + 1) * P], ident[:])
+                if half == 0:
+                    nc.scalar.activation(
+                        out=terms[:, c, 2:3], in_=sink_n[:, c : c + 1], func=EXP, bias=neg_max[c][:], scale=-1.0
+                    )
+            p_banks.append(p_ps)
+        vs_c = keep.tile([P, 4], F32, name="vs_c")
+        nc.scalar.activation(out=vs_c[:], in_=vs_ps[:, :, 0], func=COPY)
+
+        v_g1 = keep.tile([P, N], BF16, name="v_g1", tag="flipped1", align_bytes=64)
+        nc.vector.tensor_copy(v_g1[:].rearrange("p (t s) -> p s t", t=4), v_raw[1][:].indirect(offs_t[:]))
+        quantise_values(0, v_s0)
+
+        totals = keep.tile([P, 2], F32, name="totals")
+        nc.vector.reduce_sum(out=totals[:], in_=terms[:], axis=mybir.AxisListType.X)
+        recips = keep.tile([P, 2], F32, name="recips")
+        nc.vector.reciprocal(out=recips[:], in_=totals[:])
+        w_codes, w_scales = [], []
+        for c in range(2):
+            w_s = keep.tile([P, P, 4], BF16, name=f"w_s{c}", align_bytes=64)
+            nc.vector.tensor_tensor(
+                out=w_s[:],
+                in0=p_banks[c][:].rearrange("s t q -> s q t"),
+                in1=vs_c[:].unsqueeze(1).to_broadcast([P, P, 4]),
+                op=MULT,
+            )
+            codes = keep.tile([P, P], U32, name=f"w_codes{c}", align_bytes=64)
+            scales = keep.tile([P, P], U8, name=f"w_scales{c}", align_bytes=64)
+            nc.vector.quantize_mx(out=codes[:].bitcast(FP8X4), scales=scales[:], in_=w_s[:].rearrange("s q t -> s (q t)"))
+            w_codes.append(codes)
+            w_scales.append(scales)
+
+        v_s1 = interleave_values(1, turn_values(v_g1))
+        r_ps = psum.tile([P, 2, P], F32, name="r_ps", tag="recip", bufs=1)
+        for c in range(2):
+            nc.tensor.transpose(r_ps[:, c, :], recips[:, c : c + 1].to_broadcast([P, P]), ident[:])
+        recip_b = keep.tile([P, 2, P], F32, name="recip_b")
+        nc.scalar.activation(out=recip_b[:], in_=r_ps[:], func=COPY)
+
+        for h in range(2):
+            if h == 1:
+                quantise_values(1, v_s1)
+            y_banks = []
+            for c in range(2):
+                y_ps = psum.tile([P, P], F32, name="y_ps", tag=("y", "score")[h])
+                nc.tensor.matmul_mx(
+                    out=y_ps[:],
+                    lhsT=v_codes[h][:].bitcast(FP8X4),
+                    lhsT_scale=v_scales[h][:],
+                    rhs=w_codes[c][:].bitcast(FP8X4),
+                    rhs_scale=w_scales[c][:],
+                    start=True,
+                    stop=True,
+                )
+                y_banks.append(y_ps)
+            for c in range(2):
+                y = keep.tile([P, P], F32, name=f"y{h}{c}")
+                nc.scalar.activation(out=y[:], in_=y_banks[c][:], func=COPY)
+                nc.vector.tensor_tensor(
+                    placed[h][:].indirect(qoffs_t[:, c * 8 : (c + 1) * 8]), y[:], recip_b[:, c, :], MULT
+                )
+            nc.sync.dma_start(out=out[tiles[h], :], in_=placed[h][:])

@@ -6,6 +6,7 @@ from concourse.masks import make_identity
 D, T, N, NQ, DV = 512, 1024, 512, 256, 256
 P = 128
 FLOPS = 2 * NQ * N * D + 2 * NQ * N * DV
+BYTES = 4 * (2 * D * T + 2 * DV * T + T + NQ) + 2 * P * (N + NQ) // 16
 
 F32 = mybir.dt.float32
 BF16 = mybir.dt.bfloat16
@@ -15,106 +16,94 @@ U8 = mybir.dt.uint8
 FP8X4 = mybir.dt.float8_e4m3fn_x4
 
 COPY = mybir.ActivationFunctionType.Copy
+IDENTITY = mybir.ActivationFunctionType.Identity
 EXP = mybir.ActivationFunctionType.Exp
 MULT = mybir.AluOpType.mult
 MIN = mybir.AluOpType.min
 
-SCALAR_TOKENS = (384, 256)
+SCALAR_TOKENS = 352
 
 
 def tile_attend_x_router_sink_kernel(tc, xq, kT, vT, vs, sink, offs, qoffs, out):
     nc = tc.nc
     with ExitStack() as ctx:
         keep = ctx.enter_context(tc.tile_pool(name="keep", bufs=1))
-        psum = ctx.enter_context(tc.psum_pool(name="psum", bufs=2))
+        psum = ctx.enter_context(tc.psum_pool(name="psum", bufs=1))
         tiles = [slice(c * P, (c + 1) * P) for c in range(2)]
+        lists = [slice(c * 8, (c + 1) * 8) for c in range(2)]
 
         offs_t = keep.tile([P, N // 16], U16, name="offs_t")
         qoffs_t = keep.tile([P, NQ // 16], U16, name="qoffs_t")
+        sink_row = keep.tile([P, NQ], F32, name="sink_row")
+        vs_raw = keep.tile([P, T], F32, name="vs_raw")
+        nc.gpsimd.memset(sink_row[:], 0.0)
+        nc.gpsimd.memset(vs_raw[:, T // 2 :], 0.0)
+        nc.vector.memset(vs_raw[:, : T // 2], 0.0)
         k_raw = [keep.tile([P, 2, T], F32, name=f"k_raw{u}", tag=f"k_raw{u}", align_bytes=64) for u in range(2)]
         v_raw = [keep.tile([P, T], F32, name=f"v_raw{h}") for h in range(2)]
         q_raw = [keep.tile([P, T], F32, name=f"q_raw{j}") for j in range(4)]
-        vs_raw = keep.tile([P, T], F32, name="vs_raw")
         k_rows = kT.rearrange("(p j) n -> p j n", j=4)
         q_rows = xq.rearrange("(p j) n -> p j n", j=4)
-        nc.sync.dma_start(out=k_raw[0][:], in_=k_rows[:, 0:2, :])
         nc.sync.dma_start(offs_t[:], offs)
-        nc.sync.dma_start(out=v_raw[0][:], in_=vT[tiles[0], :])
-        nc.sync.dma_start(out=k_raw[1][:], in_=k_rows[:, 2:4, :])
+        nc.sync.dma_start(out=sink_row[0:1, :], in_=sink.rearrange("b q o -> b (q o)"))
+        nc.sync.dma_start(out=vs_raw[0:1, :], in_=vs[0:1, :])
+        nc.sync.dma_start(out=k_raw[0][:], in_=k_rows[:, 0:2, :])
         nc.sync.dma_start(qoffs_t[:], qoffs)
+        nc.sync.dma_start(out=k_raw[1][:], in_=k_rows[:, 2:4, :])
         for j in range(4):
             nc.sync.dma_start(out=q_raw[j][:], in_=q_rows[:, j, :])
-        nc.sync.dma_start(out=vs_raw[:], in_=vs)
-        nc.sync.dma_start(out=v_raw[1][:], in_=vT[tiles[1], :])
+        for h in range(2):
+            nc.sync.dma_start(out=v_raw[h][:], in_=vT[tiles[h], :])
 
-        sink_row = keep.tile([P, NQ], F32, name="sink_row")
-        nc.vector.memset(sink_row[:], 0.0)
-        nc.scalar.dma_start(out=sink_row[0:1, :], in_=sink.rearrange("b q o -> b (q o)"))
         ident = keep.tile([P, P], F32, name="ident")
         make_identity(nc, ident[:])
-        ident_b = keep.tile([P, P], BF16, name="ident_b")
-        make_identity(nc, ident_b[:])
         placed = [keep.tile([P, T], F32, name=f"placed{h}") for h in range(2)]
         for h in range(2):
             nc.gpsimd.memset(placed[h][:], 0.0)
         table = keep.tile([P, 1], F32, name="table")
         nc.scalar.activation(out=table[:], in_=ident[:, 0:1], func=EXP)
 
-        def turn_values(v_g):
-            v_ps = psum.tile([P, 4, P], BF16, name="v_ps", tag="turn", bufs=3)
-            for t in range(4):
-                nc.tensor.transpose(v_ps[:, t, :], v_g[:, t * P : (t + 1) * P], ident_b[:])
-            return v_ps
-
-        def interleave_values(h, v_ps):
-            v_s = keep.tile([P, P, 4], BF16, name=f"v_s{h}", align_bytes=64)
-            nc.scalar.copy(out=v_s[:], in_=v_ps[:].rearrange("s t e -> s e t"))
-            return v_s
-
-        v_codes, v_scales = [], []
-
-        def quantise_values(h, v_s):
-            codes = keep.tile([P, P], U32, name=f"v_codes{h}", tag=("flipped0", "v_codes1")[h], align_bytes=64)
-            scales = keep.tile([P, P], U8, name=f"v_scales{h}", align_bytes=64)
-            nc.vector.quantize_mx(out=codes[:].bitcast(FP8X4), scales=scales[:], in_=v_s[:].rearrange("s e t -> s (e t)"))
-            v_codes.append(codes)
-            v_scales.append(scales)
+        vs_g = keep.tile([P, N], F32, name="vs_g")
+        nc.vector.tensor_copy(vs_g[:], vs_raw[:].indirect(offs_t[:]))
+        sink_ps = psum.tile([P, 2, P], F32, name="sink_ps", tag="row")
+        for c in range(2):
+            nc.tensor.transpose(sink_ps[:, c, :], sink_row[:, tiles[c]], ident[:])
+        vs_ps = psum.tile([P, 4, P], F32, name="vs_ps", tag="value")
+        for t in range(4):
+            nc.tensor.transpose(vs_ps[:, t, :], vs_g[:, t::4], ident[:])
 
         k_g = keep.tile([P, N * 4], BF16, name="k_g", align_bytes=64)
-        k_words = k_g[:].bitcast(U32).rearrange("p (t s u) -> p s t u", t=4, u=2)
+        k_words = k_g[:].bitcast(U32).rearrange("p (s u) -> p s u", u=2)
 
         def gather_keys(u):
             k_pair = keep.tile([P, T, 2], BF16, name=f"k_pair{u}", tag="step", align_bytes=64)
             raw = k_raw[u][:].rearrange("p e n -> p n e")
-            split = SCALAR_TOKENS[u]
-            nc.scalar.activation(out=k_pair[:, :split, :], in_=raw[:, :split, :], func=COPY)
-            nc.vector.tensor_copy(out=k_pair[:, split:, :], in_=raw[:, split:, :])
+            nc.scalar.activation(out=k_pair[:, :SCALAR_TOKENS, :], in_=raw[:, :SCALAR_TOKENS, :], func=COPY)
+            nc.vector.tensor_copy(out=k_pair[:, SCALAR_TOKENS:, :], in_=raw[:, SCALAR_TOKENS:, :])
             window = k_pair[:].rearrange("p n e -> p (n e)").bitcast(U32)
-            nc.vector.tensor_copy(k_words[:, :, :, u], window.indirect(offs_t[:]))
+            nc.vector.tensor_copy(k_words[:, :, u], window.indirect(offs_t[:]))
 
         gather_keys(0)
-        v_cast = keep.tile([P, T], BF16, name="v_cast")
-        nc.scalar.activation(out=v_cast[:], in_=v_raw[0][:], func=COPY)
-        v_g0 = keep.tile([P, N], BF16, name="v_g0")
-        nc.scalar.activation(
-            out=v_g0[:].rearrange("p (t s) -> p s t", t=4), in_=v_cast[:].indirect(offs_t[:]), func=COPY
-        )
-        v_ps0 = turn_values(v_g0)
+        columns = keep.tile([P, 8], F32, name="columns", tag="k_raw0", align_bytes=64)
+        vs_c = columns[:, 0:4]
+        sink_n = columns[:, 4:6]
+        nc.scalar.activation(out=sink_n, in_=sink_ps[:, :, 0], func=COPY, scale=-1.0)
+        nc.scalar.activation(out=vs_c, in_=vs_ps[:, :, 0], func=COPY)
         gather_keys(1)
-
-        q_cast = keep.tile([P, 2, T], BF16, name="q_cast", tag="k_raw1", align_bytes=64)
-        for j in range(2):
-            nc.scalar.activation(out=q_cast[:, j, :], in_=q_raw[j][:], func=COPY)
-        q_g = keep.tile([P, NQ, 4], BF16, name="q_g", tag="step", align_bytes=64)
-        for j in range(2):
-            nc.scalar.activation(out=q_g[:, :, j], in_=q_cast[:, j, :].indirect(qoffs_t[:]), func=COPY)
         k_codes = keep.tile([P, N], U32, name="k_codes", align_bytes=64)
         k_scales = keep.tile([P, N], U8, name="k_scales", align_bytes=64)
         nc.vector.quantize_mx(out=k_codes[:].bitcast(FP8X4), scales=k_scales[:], in_=k_g[:])
-        nc.vector.tensor_copy(q_g[:, :, 2], q_raw[2][:].indirect(qoffs_t[:]))
-        v_s0 = interleave_values(0, v_ps0)
+
+        q_cast = [keep.tile([P, T], BF16, name=f"q_cast{j}", tag=f"q_cast{j}") for j in range(2)]
+        for j in range(2):
+            nc.scalar.activation(out=q_cast[j][:], in_=q_raw[j][:], func=COPY)
+        q_g = keep.tile([P, NQ, 4], BF16, name="q_g", tag="step", align_bytes=64)
         for c in range(2):
-            nc.vector.tensor_copy(q_g[:, tiles[c], 3], q_raw[3][:].indirect(qoffs_t[:, c * 8 : (c + 1) * 8]))
+            for j in range(2):
+                nc.scalar.activation(out=q_g[:, tiles[c], j], in_=q_cast[j][:].indirect(qoffs_t[:, lists[c]]), func=COPY)
+        nc.vector.tensor_copy(q_g[:, :, 2], q_raw[2][:].indirect(qoffs_t[:]))
+        for c in range(2):
+            nc.vector.tensor_copy(q_g[:, tiles[c], 3], q_raw[3][:].indirect(qoffs_t[:, lists[c]]))
         q_codes = keep.tile([P, NQ], U32, name="q_codes", align_bytes=64)
         q_scales = keep.tile([P, NQ], U8, name="q_scales", align_bytes=64)
         for cols in tiles:
@@ -122,19 +111,13 @@ def tile_attend_x_router_sink_kernel(tc, xq, kT, vT, vs, sink, offs, qoffs, out)
                 out=q_codes[:, cols].bitcast(FP8X4), scales=q_scales[:, cols], in_=q_g[:, cols, :].rearrange("p q j -> p (q j)")
             )
 
-        sink_ps = psum.tile([P, 2, P], F32, name="sink_ps", tag="y")
-        for c in range(2):
-            nc.tensor.transpose(sink_ps[:, c, :], sink_row[:, tiles[c]], ident[:])
-        sink_n = keep.tile([P, 2], F32, name="sink_n", tag="k_raw1", align_bytes=64)
-        nc.scalar.activation(out=sink_n[:], in_=sink_ps[:, :, 0], func=COPY, scale=-1.0)
-
         scores = []
-        for cols in tiles:
-            score = psum.tile([P, N], F32, name="score", tag="score")
+        for c in range(2):
+            score = psum.tile([P, N], F32, name=f"score{c}", tag=f"score{c}")
             nc.tensor.matmul_mx(
                 out=score[:],
-                lhsT=q_codes[:, cols].bitcast(FP8X4),
-                lhsT_scale=q_scales[:, cols],
+                lhsT=q_codes[:, tiles[c]].bitcast(FP8X4),
+                lhsT_scale=q_scales[:, tiles[c]],
                 rhs=k_codes[:].bitcast(FP8X4),
                 rhs_scale=k_scales[:],
                 start=True,
@@ -142,16 +125,34 @@ def tile_attend_x_router_sink_kernel(tc, xq, kT, vT, vs, sink, offs, qoffs, out)
             )
             scores.append(score)
 
-        vs_g = keep.tile([P, N], F32, name="vs_g", tag="step", align_bytes=64)
-        nc.vector.tensor_copy(vs_g[:], vs_raw[:].indirect(offs_t[:]))
-        vs_ps = psum.tile([P, 4, P], F32, name="vs_ps", tag="turn", bufs=3)
-        for t in range(4):
-            nc.tensor.transpose(vs_ps[:, t, :], vs_g[:, t::4], ident[:])
+        def gather_values(h, tag):
+            v_g = keep.tile([P, N], BF16, name=f"v_g{h}", tag=tag)
+            nc.vector.tensor_copy(v_g[:], v_raw[h][:].indirect(offs_t[:]))
+            return v_g
+
+        def turn_values(h, v_g):
+            words = v_g[:].bitcast(F32)
+            v_ps = psum.tile([P, 2, P], F32, name=f"v_ps{h}", tag="value")
+            for u in range(2):
+                nc.tensor.transpose(v_ps[:, u, :], words[:, u::2], ident[:])
+            v_s = keep.tile([P, N], BF16, name=f"v_s{h}", align_bytes=64)
+            nc.scalar.copy(
+                out=v_s[:].bitcast(F32).rearrange("s (e u) -> s e u", u=2), in_=v_ps[:].rearrange("s u e -> s e u")
+            )
+            return v_s
+
+        def quantise_values(h, v_s):
+            codes = keep.tile([P, P], U32, name=f"v_codes{h}", align_bytes=64)
+            scales = keep.tile([P, P], U8, name=f"v_scales{h}", align_bytes=64)
+            nc.vector.quantize_mx(out=codes[:].bitcast(FP8X4), scales=scales[:], in_=v_s[:])
+            return codes, scales
+
+        v_s0 = turn_values(0, gather_values(0, "q_cast1"))
 
         neg_max = []
         for c in range(2):
             least = keep.tile([P, 1], F32, name=f"neg_max{c}")
-            flipped = keep.tile([P, N], F32, name=f"flipped{c}", tag=f"flipped{c}", align_bytes=64)
+            flipped = keep.tile([P, N], F32, name=f"flipped{c}", tag=f"flipped{c}")
             nc.vector.tensor_scalar(
                 out=flipped[:],
                 in0=scores[c][:],
@@ -162,81 +163,83 @@ def tile_attend_x_router_sink_kernel(tc, xq, kT, vT, vs, sink, offs, qoffs, out)
                 accum_out=least[:],
             )
             neg_max.append(least)
+        v_g1 = gather_values(1, "flipped0")
         terms = keep.tile([P, 2, 3], F32, name="terms")
+        summed = keep.tile([P, 2, 3], F32, name="summed")
+        totals = keep.tile([P, 2], F32, name="totals")
         p_banks = []
         for c in range(2):
-            p = keep.tile([P, N], F32, name=f"p{c}")
-            p_ps = psum.tile([P, 4, P], F32, name="p_ps", tag="turn", bufs=3)
+            p = keep.tile([P, 4, P], F32, name=f"p{c}")
+            p_ps = psum.tile([P, 4, P], F32, name=f"p_ps{c}", tag=f"p{c}")
+            dealt = scores[c][:].rearrange("q (s t) -> q t s", t=4)
             for half in range(2):
-                cols = slice(half * 2 * P, (half + 1) * 2 * P)
+                places = slice(2 * half, 2 * half + 2)
                 nc.scalar.activation(
-                    out=p[:, cols],
-                    in_=scores[c][:, cols],
+                    out=p[:, places, :],
+                    in_=dealt[:, places, :],
                     func=EXP,
                     bias=neg_max[c][:],
                     scale=1.0,
                     accum_out=terms[:, c, half : half + 1],
                 )
                 for t in (2 * half, 2 * half + 1):
-                    nc.tensor.transpose(p_ps[:, t, :], p[:, t * P : (t + 1) * P], ident[:])
-                if half == 0:
-                    nc.scalar.activation(
-                        out=terms[:, c, 2:3], in_=sink_n[:, c : c + 1], func=EXP, bias=neg_max[c][:], scale=-1.0
-                    )
+                    nc.tensor.transpose(p_ps[:, t, :], p[:, t, :], ident[:])
+            nc.scalar.activation(out=terms[:, c, 2:3], in_=sink_n[:, c : c + 1], func=EXP, bias=neg_max[c][:], scale=-1.0)
+            nc.scalar.activation(out=summed[:, c, :], in_=terms[:, c, :], func=IDENTITY, accum_out=totals[:, c : c + 1])
             p_banks.append(p_ps)
-        vs_c = keep.tile([P, 4], F32, name="vs_c")
-        nc.scalar.activation(out=vs_c[:], in_=vs_ps[:, :, 0], func=COPY)
+        v_s1 = turn_values(1, v_g1)
 
-        v_g1 = keep.tile([P, N], BF16, name="v_g1", tag="flipped1", align_bytes=64)
-        nc.vector.tensor_copy(v_g1[:].rearrange("p (t s) -> p s t", t=4), v_raw[1][:].indirect(offs_t[:]))
-        quantise_values(0, v_s0)
+        w_codes = keep.tile([P, NQ], U32, name="w_codes", align_bytes=64)
+        w_scales = keep.tile([P, NQ], U8, name="w_scales", align_bytes=64)
 
-        totals = keep.tile([P, 2], F32, name="totals")
-        nc.vector.reduce_sum(out=totals[:], in_=terms[:], axis=mybir.AxisListType.X)
-        recips = keep.tile([P, 2], F32, name="recips")
-        nc.vector.reciprocal(out=recips[:], in_=totals[:])
-        w_codes, w_scales = [], []
-        for c in range(2):
+        def weigh(c):
             w_s = keep.tile([P, P, 4], BF16, name=f"w_s{c}", align_bytes=64)
             nc.vector.tensor_tensor(
                 out=w_s[:],
                 in0=p_banks[c][:].rearrange("s t q -> s q t"),
-                in1=vs_c[:].unsqueeze(1).to_broadcast([P, P, 4]),
+                in1=vs_c.unsqueeze(1).to_broadcast([P, P, 4]),
                 op=MULT,
             )
-            codes = keep.tile([P, P], U32, name=f"w_codes{c}", align_bytes=64)
-            scales = keep.tile([P, P], U8, name=f"w_scales{c}", align_bytes=64)
-            nc.vector.quantize_mx(out=codes[:].bitcast(FP8X4), scales=scales[:], in_=w_s[:].rearrange("s q t -> s (q t)"))
-            w_codes.append(codes)
-            w_scales.append(scales)
+            return w_s
 
-        v_s1 = interleave_values(1, turn_values(v_g1))
-        r_ps = psum.tile([P, 2, P], F32, name="r_ps", tag="recip", bufs=1)
+        def quantise_weights(c, w_s):
+            nc.vector.quantize_mx(
+                out=w_codes[:, tiles[c]].bitcast(FP8X4), scales=w_scales[:, tiles[c]], in_=w_s[:].rearrange("s q t -> s (q t)")
+            )
+
+        w_s0 = weigh(0)
+        v_mx0 = quantise_values(0, v_s0)
+        recips = keep.tile([P, 2], F32, name="recips")
+        nc.vector.reciprocal(out=recips[:], in_=totals[:])
+        quantise_weights(0, w_s0)
+        w_s1 = weigh(1)
+        v_mx1 = quantise_values(1, v_s1)
+        quantise_weights(1, w_s1)
+
+        r_ps = psum.tile([P, 2, P], F32, name="r_ps", tag="row")
         for c in range(2):
             nc.tensor.transpose(r_ps[:, c, :], recips[:, c : c + 1].to_broadcast([P, P]), ident[:])
-        recip_b = keep.tile([P, 2, P], F32, name="recip_b")
-        nc.scalar.activation(out=recip_b[:], in_=r_ps[:], func=COPY)
+        recip_b = keep.tile([P, NQ], F32, name="recip_b")
+        nc.scalar.activation(out=recip_b[:], in_=r_ps[:].rearrange("p c q -> p (c q)"), func=COPY)
 
-        for h in range(2):
-            if h == 1:
-                quantise_values(1, v_s1)
-            y_banks = []
-            for c in range(2):
-                y_ps = psum.tile([P, P], F32, name="y_ps", tag=("y", "score")[h])
-                nc.tensor.matmul_mx(
-                    out=y_ps[:],
-                    lhsT=v_codes[h][:].bitcast(FP8X4),
-                    lhsT_scale=v_scales[h][:],
-                    rhs=w_codes[c][:].bitcast(FP8X4),
-                    rhs_scale=w_scales[c][:],
-                    start=True,
-                    stop=True,
-                )
-                y_banks.append(y_ps)
-            for c in range(2):
-                y = keep.tile([P, P], F32, name=f"y{h}{c}")
-                nc.scalar.activation(out=y[:], in_=y_banks[c][:], func=COPY)
-                nc.vector.tensor_tensor(
-                    placed[h][:].indirect(qoffs_t[:, c * 8 : (c + 1) * 8]), y[:], recip_b[:, c, :], MULT
-                )
-            nc.sync.dma_start(out=out[tiles[h], :], in_=placed[h][:])
+        def finish(h, v_mx, cols, entries, tag):
+            width = cols.stop - cols.start
+            y_ps = psum.tile([P, width], F32, name=f"y_ps_{tag}", tag=tag)
+            nc.tensor.matmul_mx(
+                out=y_ps[:],
+                lhsT=v_mx[0][:].bitcast(FP8X4),
+                lhsT_scale=v_mx[1][:],
+                rhs=w_codes[:, cols].bitcast(FP8X4),
+                rhs_scale=w_scales[:, cols],
+                start=True,
+                stop=True,
+            )
+            y = keep.tile([P, width], F32, name=f"y_{tag}")
+            nc.scalar.activation(out=y[:], in_=y_ps[:], func=COPY)
+            nc.vector.tensor_tensor(placed[h][:].indirect(qoffs_t[:, entries]), y[:], recip_b[:, cols], MULT)
+
+        for c in range(2):
+            finish(0, v_mx0, tiles[c], lists[c], f"y{c}")
+        nc.sync.dma_start(out=out[tiles[0], :], in_=placed[0][:])
+        finish(1, v_mx1, slice(0, NQ), slice(0, NQ // 16), "score0")
+        nc.sync.dma_start(out=out[tiles[1], :], in_=placed[1][:])

@@ -5,6 +5,7 @@ from concourse.masks import make_identity
 
 D, T, N, NQ, DV = 512, 1024, 512, 256, 256
 P = 128
+LAST = P - 1
 FLOPS = 2 * NQ * N * D + 2 * NQ * N * DV
 BYTES = 4 * (2 * D * T + 2 * DV * T + T + NQ) + 2 * P * (N + NQ) // 16
 
@@ -36,17 +37,16 @@ def tile_attend_x_router_sink_kernel(tc, xq, kT, vT, vs, sink, offs, qoffs, out)
         qoffs_t = keep.tile([P, NQ // 16], U16, name="qoffs_t")
         sink_row = keep.tile([P, NQ], F32, name="sink_row")
         vs_raw = keep.tile([P, T], F32, name="vs_raw")
-        nc.gpsimd.memset(sink_row[:], 0.0)
-        nc.gpsimd.memset(vs_raw[:, T // 2 :], 0.0)
-        nc.vector.memset(vs_raw[:, : T // 2], 0.0)
+        nc.vector.memset(vs_raw[:LAST, :], 0.0)
+        nc.vector.memset(sink_row[:LAST, :], 0.0)
+        nc.scalar.dma_start(out=sink_row[LAST:, :], in_=sink.rearrange("b q o -> b (q o)"))
         k_raw = [keep.tile([P, 2, T], F32, name=f"k_raw{u}", tag=f"k_raw{u}", align_bytes=64) for u in range(2)]
-        v_raw = [keep.tile([P, T], F32, name=f"v_raw{h}") for h in range(2)]
+        v_raw = [keep.tile([P, T], F32, name=f"v_raw{h}", tag=f"v_raw{h}") for h in range(2)]
         q_raw = [keep.tile([P, T], F32, name=f"q_raw{j}") for j in range(4)]
         k_rows = kT.rearrange("(p j) n -> p j n", j=4)
         q_rows = xq.rearrange("(p j) n -> p j n", j=4)
         nc.sync.dma_start(offs_t[:], offs)
-        nc.sync.dma_start(out=sink_row[0:1, :], in_=sink.rearrange("b q o -> b (q o)"))
-        nc.sync.dma_start(out=vs_raw[0:1, :], in_=vs[0:1, :])
+        nc.sync.dma_start(out=vs_raw[LAST:, :], in_=vs[0:1, :])
         nc.sync.dma_start(out=k_raw[0][:], in_=k_rows[:, 0:2, :])
         nc.sync.dma_start(qoffs_t[:], qoffs)
         nc.sync.dma_start(out=k_raw[1][:], in_=k_rows[:, 2:4, :])
@@ -59,57 +59,51 @@ def tile_attend_x_router_sink_kernel(tc, xq, kT, vT, vs, sink, offs, qoffs, out)
         make_identity(nc, ident[:])
         placed = [keep.tile([P, T], F32, name=f"placed{h}") for h in range(2)]
         for h in range(2):
-            nc.gpsimd.memset(placed[h][:], 0.0)
+            (nc.gpsimd, nc.vector)[h].memset(placed[h][:], 0.0)
         table = keep.tile([P, 1], F32, name="table")
         nc.scalar.activation(out=table[:], in_=ident[:, 0:1], func=EXP)
 
         vs_g = keep.tile([P, N], F32, name="vs_g")
         nc.vector.tensor_copy(vs_g[:], vs_raw[:].indirect(offs_t[:]))
-        sink_ps = psum.tile([P, 2, P], F32, name="sink_ps", tag="row")
-        for c in range(2):
-            nc.tensor.transpose(sink_ps[:, c, :], sink_row[:, tiles[c]], ident[:])
         vs_ps = psum.tile([P, 4, P], F32, name="vs_ps", tag="value")
         for t in range(4):
             nc.tensor.transpose(vs_ps[:, t, :], vs_g[:, t::4], ident[:])
+        sink_ps = psum.tile([P, 2, P], F32, name="sink_ps", tag="row")
+        for c in range(2):
+            nc.tensor.transpose(sink_ps[:, c, :], sink_row[:, tiles[c]], ident[:])
 
         k_g = keep.tile([P, N * 4], BF16, name="k_g", align_bytes=64)
-        k_words = k_g[:].bitcast(U32).rearrange("p (s u) -> p s u", u=2)
+        k_words = k_g[:].bitcast(U32).rearrange("p (t s u) -> p s t u", t=4, u=2)
 
         def gather_keys(u):
-            k_pair = keep.tile([P, T, 2], BF16, name=f"k_pair{u}", tag="step", align_bytes=64)
+            k_pair = keep.tile([P, T, 2], BF16, name=f"k_pair{u}", align_bytes=64)
             raw = k_raw[u][:].rearrange("p e n -> p n e")
             nc.scalar.activation(out=k_pair[:, :SCALAR_TOKENS, :], in_=raw[:, :SCALAR_TOKENS, :], func=COPY)
             nc.vector.tensor_copy(out=k_pair[:, SCALAR_TOKENS:, :], in_=raw[:, SCALAR_TOKENS:, :])
             window = k_pair[:].rearrange("p n e -> p (n e)").bitcast(U32)
-            nc.vector.tensor_copy(k_words[:, :, u], window.indirect(offs_t[:]))
+            nc.vector.tensor_copy(k_words[:, :, :, u], window.indirect(offs_t[:]))
 
         gather_keys(0)
         columns = keep.tile([P, 8], F32, name="columns", tag="k_raw0", align_bytes=64)
         vs_c = columns[:, 0:4]
         sink_n = columns[:, 4:6]
-        nc.scalar.activation(out=sink_n, in_=sink_ps[:, :, 0], func=COPY, scale=-1.0)
-        nc.scalar.activation(out=vs_c, in_=vs_ps[:, :, 0], func=COPY)
+        nc.scalar.activation(out=sink_n, in_=sink_ps[:, :, LAST], func=COPY, scale=-1.0)
+        nc.scalar.activation(out=vs_c, in_=vs_ps[:, :, LAST], func=COPY)
         gather_keys(1)
         k_codes = keep.tile([P, N], U32, name="k_codes", align_bytes=64)
         k_scales = keep.tile([P, N], U8, name="k_scales", align_bytes=64)
         nc.vector.quantize_mx(out=k_codes[:].bitcast(FP8X4), scales=k_scales[:], in_=k_g[:])
 
         q_cast = [keep.tile([P, T], BF16, name=f"q_cast{j}", tag=f"q_cast{j}") for j in range(2)]
+        q_g = keep.tile([P, NQ, 4], BF16, name="q_g", align_bytes=64)
         for j in range(2):
             nc.scalar.activation(out=q_cast[j][:], in_=q_raw[j][:], func=COPY)
-        q_g = keep.tile([P, NQ, 4], BF16, name="q_g", tag="step", align_bytes=64)
-        for c in range(2):
-            for j in range(2):
-                nc.scalar.activation(out=q_g[:, tiles[c], j], in_=q_cast[j][:].indirect(qoffs_t[:, lists[c]]), func=COPY)
-        nc.vector.tensor_copy(q_g[:, :, 2], q_raw[2][:].indirect(qoffs_t[:]))
-        for c in range(2):
-            nc.vector.tensor_copy(q_g[:, tiles[c], 3], q_raw[3][:].indirect(qoffs_t[:, lists[c]]))
+            nc.scalar.activation(out=q_g[:, :, j], in_=q_cast[j][:].indirect(qoffs_t[:]), func=COPY)
+        for j in range(2, 4):
+            nc.vector.tensor_copy(q_g[:, :, j], q_raw[j][:].indirect(qoffs_t[:]))
         q_codes = keep.tile([P, NQ], U32, name="q_codes", align_bytes=64)
         q_scales = keep.tile([P, NQ], U8, name="q_scales", align_bytes=64)
-        for cols in tiles:
-            nc.vector.quantize_mx(
-                out=q_codes[:, cols].bitcast(FP8X4), scales=q_scales[:, cols], in_=q_g[:, cols, :].rearrange("p q j -> p (q j)")
-            )
+        nc.vector.quantize_mx(out=q_codes[:].bitcast(FP8X4), scales=q_scales[:], in_=q_g[:].rearrange("p q j -> p (q j)"))
 
         scores = []
         for c in range(2):
@@ -125,17 +119,20 @@ def tile_attend_x_router_sink_kernel(tc, xq, kT, vT, vs, sink, offs, qoffs, out)
             )
             scores.append(score)
 
-        def gather_values(h, tag):
-            v_g = keep.tile([P, N], BF16, name=f"v_g{h}", tag=tag)
+        def gather_values(h):
+            v_g = keep.tile([P, N], BF16, name=f"v_g{h}")
             nc.vector.tensor_copy(v_g[:], v_raw[h][:].indirect(offs_t[:]))
             return v_g
 
-        def turn_values(h, v_g):
+        def turn_values(h, v_g, tag):
             words = v_g[:].bitcast(F32)
-            v_ps = psum.tile([P, 2, P], F32, name=f"v_ps{h}", tag="value")
+            v_ps = psum.tile([P, 2, P], F32, name=f"v_ps{h}", tag=tag)
             for u in range(2):
                 nc.tensor.transpose(v_ps[:, u, :], words[:, u::2], ident[:])
-            v_s = keep.tile([P, N], BF16, name=f"v_s{h}", align_bytes=64)
+            return v_ps
+
+        def interleave_values(h, v_ps):
+            v_s = keep.tile([P, N], BF16, name=f"v_s{h}", tag=f"neg_max{h}", align_bytes=64)
             nc.scalar.copy(
                 out=v_s[:].bitcast(F32).rearrange("s (e u) -> s e u", u=2), in_=v_ps[:].rearrange("s u e -> s e u")
             )
@@ -147,14 +144,14 @@ def tile_attend_x_router_sink_kernel(tc, xq, kT, vT, vs, sink, offs, qoffs, out)
             nc.vector.quantize_mx(out=codes[:].bitcast(FP8X4), scales=scales[:], in_=v_s[:])
             return codes, scales
 
-        v_s0 = turn_values(0, gather_values(0, "q_cast1"))
+        v_ps0 = turn_values(0, gather_values(0), "value")
 
         neg_max = []
+        flipped = keep.tile([P, 2, N], F32, name="flipped", tag="v_raw0")
         for c in range(2):
-            least = keep.tile([P, 1], F32, name=f"neg_max{c}")
-            flipped = keep.tile([P, N], F32, name=f"flipped{c}", tag=f"flipped{c}")
+            least = keep.tile([P, 1], F32, name=f"neg_max{c}", tag=f"neg_max{c}", align_bytes=64)
             nc.vector.tensor_scalar(
-                out=flipped[:],
+                out=flipped[:, c, :],
                 in0=scores[c][:],
                 scalar1=-1.0,
                 scalar2=sink_n[:, c : c + 1],
@@ -163,15 +160,15 @@ def tile_attend_x_router_sink_kernel(tc, xq, kT, vT, vs, sink, offs, qoffs, out)
                 accum_out=least[:],
             )
             neg_max.append(least)
-        v_g1 = gather_values(1, "flipped0")
+        v_g1 = gather_values(1)
         terms = keep.tile([P, 2, 3], F32, name="terms")
         summed = keep.tile([P, 2, 3], F32, name="summed")
         totals = keep.tile([P, 2], F32, name="totals")
         p_banks = []
         for c in range(2):
-            p = keep.tile([P, 4, P], F32, name=f"p{c}")
+            p = keep.tile([P, 4, P], F32, name=f"p{c}", tag=f"p_sb{c}")
             p_ps = psum.tile([P, 4, P], F32, name=f"p_ps{c}", tag=f"p{c}")
-            dealt = scores[c][:].rearrange("q (s t) -> q t s", t=4)
+            dealt = scores[c][:].rearrange("q (t s) -> q t s", t=4)
             for half in range(2):
                 places = slice(2 * half, 2 * half + 2)
                 nc.scalar.activation(
@@ -184,10 +181,15 @@ def tile_attend_x_router_sink_kernel(tc, xq, kT, vT, vs, sink, offs, qoffs, out)
                 )
                 for t in (2 * half, 2 * half + 1):
                     nc.tensor.transpose(p_ps[:, t, :], p[:, t, :], ident[:])
-            nc.scalar.activation(out=terms[:, c, 2:3], in_=sink_n[:, c : c + 1], func=EXP, bias=neg_max[c][:], scale=-1.0)
+                if half == 0:
+                    nc.scalar.activation(
+                        out=terms[:, c, 2:3], in_=sink_n[:, c : c + 1], func=EXP, bias=neg_max[c][:], scale=-1.0
+                    )
             nc.scalar.activation(out=summed[:, c, :], in_=terms[:, c, :], func=IDENTITY, accum_out=totals[:, c : c + 1])
+            if c == 0:
+                v_s0 = interleave_values(0, v_ps0)
             p_banks.append(p_ps)
-        v_s1 = turn_values(1, v_g1)
+        v_ps1 = turn_values(1, v_g1, "score1")
 
         w_codes = keep.tile([P, NQ], U32, name="w_codes", align_bytes=64)
         w_scales = keep.tile([P, NQ], U8, name="w_scales", align_bytes=64)
@@ -207,22 +209,16 @@ def tile_attend_x_router_sink_kernel(tc, xq, kT, vT, vs, sink, offs, qoffs, out)
                 out=w_codes[:, tiles[c]].bitcast(FP8X4), scales=w_scales[:, tiles[c]], in_=w_s[:].rearrange("s q t -> s (q t)")
             )
 
-        w_s0 = weigh(0)
-        v_mx0 = quantise_values(0, v_s0)
-        recips = keep.tile([P, 2], F32, name="recips")
-        nc.vector.reciprocal(out=recips[:], in_=totals[:])
-        quantise_weights(0, w_s0)
-        w_s1 = weigh(1)
-        v_mx1 = quantise_values(1, v_s1)
-        quantise_weights(1, w_s1)
-
-        r_ps = psum.tile([P, 2, P], F32, name="r_ps", tag="row")
-        for c in range(2):
-            nc.tensor.transpose(r_ps[:, c, :], recips[:, c : c + 1].to_broadcast([P, P]), ident[:])
         recip_b = keep.tile([P, NQ], F32, name="recip_b")
-        nc.scalar.activation(out=recip_b[:], in_=r_ps[:].rearrange("p c q -> p (c q)"), func=COPY)
 
-        def finish(h, v_mx, cols, entries, tag):
+        def spread_reciprocals(c):
+            recip = keep.tile([P, 1], F32, name=f"recip{c}", tag=("recip0", "p_sb1")[c])
+            nc.vector.reciprocal(out=recip[:], in_=totals[:, c : c + 1])
+            r_ps = psum.tile([P, P], F32, name=f"r_ps{c}", tag=("row", "value")[c])
+            nc.tensor.transpose(r_ps[:], recip[:].to_broadcast([P, P]), ident[:])
+            nc.scalar.activation(out=recip_b[:, tiles[c]], in_=r_ps[:], func=COPY)
+
+        def multiply(v_mx, cols, tag):
             width = cols.stop - cols.start
             y_ps = psum.tile([P, width], F32, name=f"y_ps_{tag}", tag=tag)
             nc.tensor.matmul_mx(
@@ -236,10 +232,23 @@ def tile_attend_x_router_sink_kernel(tc, xq, kT, vT, vs, sink, offs, qoffs, out)
             )
             y = keep.tile([P, width], F32, name=f"y_{tag}")
             nc.scalar.activation(out=y[:], in_=y_ps[:], func=COPY)
+            return y
+
+        def place(h, y, cols, entries):
             nc.vector.tensor_tensor(placed[h][:].indirect(qoffs_t[:, entries]), y[:], recip_b[:, cols], MULT)
 
-        for c in range(2):
-            finish(0, v_mx0, tiles[c], lists[c], f"y{c}")
+        spread_reciprocals(0)
+        w_s0 = weigh(0)
+        v_mx0 = quantise_values(0, v_s0)
+        quantise_weights(0, w_s0)
+        y_first = multiply(v_mx0, tiles[0], "y0")
+        w_s1 = weigh(1)
+        spread_reciprocals(1)
+        quantise_weights(1, w_s1)
+        y_second = multiply(v_mx0, tiles[1], "y1")
+        place(0, y_first, tiles[0], lists[0])
+        v_mx1 = quantise_values(1, interleave_values(1, v_ps1))
+        place(0, y_second, tiles[1], lists[1])
         nc.sync.dma_start(out=out[tiles[0], :], in_=placed[0][:])
-        finish(1, v_mx1, slice(0, NQ), slice(0, NQ // 16), "score0")
+        place(1, multiply(v_mx1, slice(0, NQ), "score0"), slice(0, NQ), slice(0, NQ // 16))
         nc.sync.dma_start(out=out[tiles[1], :], in_=placed[1][:])

@@ -39,16 +39,17 @@ def tile_attend_x_router_sink_kernel(tc, xq, kT, vT, vs, sink, offs, qoffs, out)
         vs_raw = keep.tile([P, T], F32, name="vs_raw")
         nc.vector.memset(vs_raw[:LAST, :], 0.0)
         nc.vector.memset(sink_row[:LAST, :], 0.0)
-        nc.scalar.dma_start(out=sink_row[LAST:, :], in_=sink.rearrange("b q o -> b (q o)"))
         k_raw = [keep.tile([P, 2, T], F32, name=f"k_raw{u}", tag=f"k_raw{u}", align_bytes=64) for u in range(2)]
         v_raw = [keep.tile([P, T], F32, name=f"v_raw{h}", tag=f"v_raw{h}") for h in range(2)]
         q_raw = [keep.tile([P, T], F32, name=f"q_raw{j}") for j in range(4)]
         k_rows = kT.rearrange("(p j) n -> p j n", j=4)
         q_rows = xq.rearrange("(p j) n -> p j n", j=4)
+        nc.sync.dma_start(out=k_raw[0][:, 0, :], in_=k_rows[:, 0, :])
         nc.sync.dma_start(offs_t[:], offs)
         nc.sync.dma_start(out=vs_raw[LAST:, :], in_=vs[0:1, :])
-        nc.sync.dma_start(out=k_raw[0][:], in_=k_rows[:, 0:2, :])
+        nc.sync.dma_start(out=k_raw[0][:, 1, :], in_=k_rows[:, 1, :])
         nc.sync.dma_start(qoffs_t[:], qoffs)
+        nc.sync.dma_start(out=sink_row[LAST:, :], in_=sink.rearrange("b q o -> b (q o)"))
         nc.sync.dma_start(out=k_raw[1][:], in_=k_rows[:, 2:4, :])
         for j in range(4):
             nc.sync.dma_start(out=q_raw[j][:], in_=q_rows[:, j, :])
@@ -61,7 +62,7 @@ def tile_attend_x_router_sink_kernel(tc, xq, kT, vT, vs, sink, offs, qoffs, out)
         for h in range(2):
             (nc.gpsimd, nc.vector)[h].memset(placed[h][:], 0.0)
         table = keep.tile([P, 1], F32, name="table")
-        nc.scalar.activation(out=table[:], in_=ident[:, 0:1], func=EXP)
+        nc.scalar.activation(out=table[:LAST, :], in_=sink_row[:LAST, 0:1], func=EXP)
 
         vs_g = keep.tile([P, N], F32, name="vs_g")
         nc.vector.tensor_copy(vs_g[:], vs_raw[:].indirect(offs_t[:]))
@@ -76,7 +77,7 @@ def tile_attend_x_router_sink_kernel(tc, xq, kT, vT, vs, sink, offs, qoffs, out)
         k_words = k_g[:].bitcast(U32).rearrange("p (t s u) -> p s t u", t=4, u=2)
 
         def gather_keys(u):
-            k_pair = keep.tile([P, T, 2], BF16, name=f"k_pair{u}", align_bytes=64)
+            k_pair = keep.tile([P, T, 2], BF16, name=f"k_pair{u}", tag=f"k_pair{u}", align_bytes=64)
             raw = k_raw[u][:].rearrange("p e n -> p n e")
             nc.scalar.activation(out=k_pair[:, :SCALAR_TOKENS, :], in_=raw[:, :SCALAR_TOKENS, :], func=COPY)
             nc.vector.tensor_copy(out=k_pair[:, SCALAR_TOKENS:, :], in_=raw[:, SCALAR_TOKENS:, :])
@@ -94,11 +95,11 @@ def tile_attend_x_router_sink_kernel(tc, xq, kT, vT, vs, sink, offs, qoffs, out)
         k_scales = keep.tile([P, N], U8, name="k_scales", align_bytes=64)
         nc.vector.quantize_mx(out=k_codes[:].bitcast(FP8X4), scales=k_scales[:], in_=k_g[:])
 
-        q_cast = [keep.tile([P, T], BF16, name=f"q_cast{j}", tag=f"q_cast{j}") for j in range(2)]
-        q_g = keep.tile([P, NQ, 4], BF16, name="q_g", align_bytes=64)
+        q_cast = keep.tile([P, 2, T], BF16, name="q_cast", tag="k_raw1", align_bytes=64)
+        q_g = keep.tile([P, NQ, 4], BF16, name="q_g", tag="k_pair1", align_bytes=64)
         for j in range(2):
-            nc.scalar.activation(out=q_cast[j][:], in_=q_raw[j][:], func=COPY)
-            nc.scalar.activation(out=q_g[:, :, j], in_=q_cast[j][:].indirect(qoffs_t[:]), func=COPY)
+            nc.scalar.activation(out=q_cast[:, j, :], in_=q_raw[j][:], func=COPY)
+            nc.scalar.activation(out=q_g[:, :, j], in_=q_cast[:, j, :].indirect(qoffs_t[:]), func=COPY)
         for j in range(2, 4):
             nc.vector.tensor_copy(q_g[:, :, j], q_raw[j][:].indirect(qoffs_t[:]))
         q_codes = keep.tile([P, NQ], U32, name="q_codes", align_bytes=64)
@@ -120,7 +121,7 @@ def tile_attend_x_router_sink_kernel(tc, xq, kT, vT, vs, sink, offs, qoffs, out)
             scores.append(score)
 
         def gather_values(h):
-            v_g = keep.tile([P, N], BF16, name=f"v_g{h}")
+            v_g = keep.tile([P, N], BF16, name=f"v_g{h}", tag=("k_raw1", "v_g1")[h], align_bytes=64)
             nc.vector.tensor_copy(v_g[:], v_raw[h][:].indirect(offs_t[:]))
             return v_g
 
@@ -197,9 +198,9 @@ def tile_attend_x_router_sink_kernel(tc, xq, kT, vT, vs, sink, offs, qoffs, out)
         def weigh(c):
             w_s = keep.tile([P, P, 4], BF16, name=f"w_s{c}", align_bytes=64)
             nc.vector.tensor_tensor(
-                out=w_s[:],
-                in0=p_banks[c][:].rearrange("s t q -> s q t"),
-                in1=vs_c.unsqueeze(1).to_broadcast([P, P, 4]),
+                out=w_s[:].rearrange("s (g i) t -> s g t i", i=4),
+                in0=p_banks[c][:].rearrange("s t (g i) -> s g t i", i=4),
+                in1=vs_c.unsqueeze(1).unsqueeze(3).to_broadcast([P, P // 4, 4, 4]),
                 op=MULT,
             )
             return w_s

@@ -198,9 +198,9 @@ def tile_attend_x_router_sink_kernel(tc, xq, kT, vT, vs, sink, offs, qoffs, out)
         def weigh(c):
             w_s = keep.tile([P, P, 4], BF16, name=f"w_s{c}", align_bytes=64)
             nc.vector.tensor_tensor(
-                out=w_s[:].rearrange("s (g i) t -> s g t i", i=4),
-                in0=p_banks[c][:].rearrange("s t (g i) -> s g t i", i=4),
-                in1=vs_c.unsqueeze(1).unsqueeze(3).to_broadcast([P, P // 4, 4, 4]),
+                out=w_s[:],
+                in0=p_banks[c][:].rearrange("s t q -> s q t"),
+                in1=vs_c.unsqueeze(1).to_broadcast([P, P, 4]),
                 op=MULT,
             )
             return w_s

@@ -39,18 +39,19 @@ def tile_attend_x_router_sink_kernel(tc, xq, kT, vT, vs, sink, offs, qoffs, out)
         vs_raw = keep.tile([P, T], F32, name="vs_raw")
         nc.vector.memset(vs_raw[:LAST, :], 0.0)
         nc.vector.memset(sink_row[:LAST, :], 0.0)
-        k_raw = [keep.tile([P, 2, T], F32, name=f"k_raw{u}", tag=f"k_raw{u}", align_bytes=64) for u in range(2)]
-        v_raw = [keep.tile([P, T], F32, name=f"v_raw{h}", tag=f"v_raw{h}") for h in range(2)]
+        k_plane = [keep.tile([P, T], F32, name=f"k_plane{j}") for j in range(2)]
+        k_raw = keep.tile([P, 2, T], F32, name="k_raw", tag="k_raw1", align_bytes=64)
+        v_raw = [keep.tile([P, T], F32, name=f"v_raw{h}", tag=f"v_raw{h}", align_bytes=64) for h in range(2)]
         q_raw = [keep.tile([P, T], F32, name=f"q_raw{j}") for j in range(4)]
         k_rows = kT.rearrange("(p j) n -> p j n", j=4)
         q_rows = xq.rearrange("(p j) n -> p j n", j=4)
-        nc.sync.dma_start(out=k_raw[0][:, 0, :], in_=k_rows[:, 0, :])
         nc.sync.dma_start(offs_t[:], offs)
         nc.sync.dma_start(out=vs_raw[LAST:, :], in_=vs[0:1, :])
-        nc.sync.dma_start(out=k_raw[0][:, 1, :], in_=k_rows[:, 1, :])
+        for j in range(2):
+            nc.sync.dma_start(out=k_plane[j][:], in_=k_rows[:, j, :])
         nc.sync.dma_start(qoffs_t[:], qoffs)
         nc.sync.dma_start(out=sink_row[LAST:, :], in_=sink.rearrange("b q o -> b (q o)"))
-        nc.sync.dma_start(out=k_raw[1][:], in_=k_rows[:, 2:4, :])
+        nc.sync.dma_start(out=k_raw[:], in_=k_rows[:, 2:4, :])
         for j in range(4):
             nc.sync.dma_start(out=q_raw[j][:], in_=q_rows[:, j, :])
         for h in range(2):
@@ -74,23 +75,21 @@ def tile_attend_x_router_sink_kernel(tc, xq, kT, vT, vs, sink, offs, qoffs, out)
             nc.tensor.transpose(sink_ps[:, c, :], sink_row[:, tiles[c]], ident[:])
 
         k_g = keep.tile([P, N * 4], BF16, name="k_g", align_bytes=64)
-        k_words = k_g[:].bitcast(U32).rearrange("p (t s u) -> p s t u", t=4, u=2)
-
-        def gather_keys(u):
-            k_pair = keep.tile([P, T, 2], BF16, name=f"k_pair{u}", tag=f"k_pair{u}", align_bytes=64)
-            raw = k_raw[u][:].rearrange("p e n -> p n e")
-            nc.scalar.activation(out=k_pair[:, :SCALAR_TOKENS, :], in_=raw[:, :SCALAR_TOKENS, :], func=COPY)
-            nc.vector.tensor_copy(out=k_pair[:, SCALAR_TOKENS:, :], in_=raw[:, SCALAR_TOKENS:, :])
-            window = k_pair[:].rearrange("p n e -> p (n e)").bitcast(U32)
-            nc.vector.tensor_copy(k_words[:, :, :, u], window.indirect(offs_t[:]))
-
-        gather_keys(0)
-        columns = keep.tile([P, 8], F32, name="columns", tag="k_raw0", align_bytes=64)
+        k_places = k_g[:].rearrange("p (t s j) -> p s t j", t=4, j=4)
+        for j in range(2):
+            nc.vector.tensor_copy(k_places[:, :, :, j], k_plane[j][:].indirect(offs_t[:]))
+        columns = keep.tile([P, 8], F32, name="columns")
         vs_c = columns[:, 0:4]
         sink_n = columns[:, 4:6]
-        nc.scalar.activation(out=sink_n, in_=sink_ps[:, :, LAST], func=COPY, scale=-1.0)
         nc.scalar.activation(out=vs_c, in_=vs_ps[:, :, LAST], func=COPY)
-        gather_keys(1)
+        nc.scalar.activation(out=sink_n, in_=sink_ps[:, :, LAST], func=COPY, scale=-1.0)
+        k_pair = keep.tile([P, T, 2], BF16, name="k_pair", tag="k_pair1", align_bytes=64)
+        raw = k_raw[:].rearrange("p e n -> p n e")
+        nc.scalar.activation(out=k_pair[:, :SCALAR_TOKENS, :], in_=raw[:, :SCALAR_TOKENS, :], func=COPY)
+        nc.vector.tensor_copy(out=k_pair[:, SCALAR_TOKENS:, :], in_=raw[:, SCALAR_TOKENS:, :])
+        k_words = k_g[:].bitcast(U32).rearrange("p (t s u) -> p s t u", t=4, u=2)
+        window = k_pair[:].rearrange("p n e -> p (n e)").bitcast(U32)
+        nc.vector.tensor_copy(k_words[:, :, :, 1], window.indirect(offs_t[:]))
         k_codes = keep.tile([P, N], U32, name="k_codes", align_bytes=64)
         k_scales = keep.tile([P, N], U8, name="k_scales", align_bytes=64)
         nc.vector.quantize_mx(out=k_codes[:].bitcast(FP8X4), scales=k_scales[:], in_=k_g[:])
@@ -120,10 +119,7 @@ def tile_attend_x_router_sink_kernel(tc, xq, kT, vT, vs, sink, offs, qoffs, out)
             )
             scores.append(score)
 
-        def gather_values(h):
-            v_g = keep.tile([P, N], BF16, name=f"v_g{h}", tag=("k_raw1", "v_g1")[h], align_bytes=64)
-            nc.vector.tensor_copy(v_g[:], v_raw[h][:].indirect(offs_t[:]))
-            return v_g
+        v_g0 = keep.tile([P, N], BF16, name="v_g0", tag="k_raw1", align_bytes=64)
 
         def turn_values(h, v_g, tag):
             words = v_g[:].bitcast(F32)
@@ -145,10 +141,14 @@ def tile_attend_x_router_sink_kernel(tc, xq, kT, vT, vs, sink, offs, qoffs, out)
             nc.vector.quantize_mx(out=codes[:].bitcast(FP8X4), scales=scales[:], in_=v_s[:])
             return codes, scales
 
-        v_ps0 = turn_values(0, gather_values(0), "value")
+        v_cast = keep.tile([P, T], BF16, name="v_cast", tag="v_cast", align_bytes=64)
+        nc.scalar.activation(out=v_cast[:], in_=v_raw[0][:], func=COPY)
+        nc.vector.tensor_copy(v_g0[:, : N // 2], v_raw[0][:].indirect(offs_t[:, : N // 32]))
+        nc.scalar.activation(out=v_g0[:, N // 2 :], in_=v_cast[:].indirect(offs_t[:, N // 32 :]), func=COPY)
+        v_ps0 = turn_values(0, v_g0, "value")
 
         neg_max = []
-        flipped = keep.tile([P, 2, N], F32, name="flipped", tag="v_raw0")
+        flipped = keep.tile([P, 2, N], F32, name="flipped", tag="v_raw0", align_bytes=64)
         for c in range(2):
             least = keep.tile([P, 1], F32, name=f"neg_max{c}", tag=f"neg_max{c}", align_bytes=64)
             nc.vector.tensor_scalar(
@@ -161,7 +161,8 @@ def tile_attend_x_router_sink_kernel(tc, xq, kT, vT, vs, sink, offs, qoffs, out)
                 accum_out=least[:],
             )
             neg_max.append(least)
-        v_g1 = gather_values(1)
+        v_g1 = keep.tile([P, N], BF16, name="v_g1", tag="v_cast", align_bytes=64)
+        nc.vector.tensor_copy(v_g1[:], v_raw[1][:].indirect(offs_t[:]))
         terms = keep.tile([P, 2, 3], F32, name="terms")
         summed = keep.tile([P, 2, 3], F32, name="summed")
         totals = keep.tile([P, 2], F32, name="totals")

@@ -22,8 +22,6 @@ EXP = mybir.ActivationFunctionType.Exp
 MULT = mybir.AluOpType.mult
 MIN = mybir.AluOpType.min
 
-SCALAR_TOKENS = 352
-
 
 def tile_attend_x_router_sink_kernel(tc, xq, kT, vT, vs, sink, offs, qoffs, out):
     nc = tc.nc
@@ -39,8 +37,7 @@ def tile_attend_x_router_sink_kernel(tc, xq, kT, vT, vs, sink, offs, qoffs, out)
         vs_raw = keep.tile([P, T], F32, name="vs_raw")
         nc.vector.memset(vs_raw[:LAST, :], 0.0)
         nc.vector.memset(sink_row[:LAST, :], 0.0)
-        k_plane = [keep.tile([P, T], F32, name=f"k_plane{j}") for j in range(2)]
-        k_raw = keep.tile([P, 2, T], F32, name="k_raw", tag="k_raw1", align_bytes=64)
+        k_raw = [keep.tile([P, T], F32, name=f"k_raw{j}") for j in range(4)]
         v_raw = [keep.tile([P, T], F32, name=f"v_raw{h}", tag=f"v_raw{h}", align_bytes=64) for h in range(2)]
         q_raw = [keep.tile([P, T], F32, name=f"q_raw{j}") for j in range(4)]
         k_rows = kT.rearrange("(p j) n -> p j n", j=4)
@@ -48,10 +45,11 @@ def tile_attend_x_router_sink_kernel(tc, xq, kT, vT, vs, sink, offs, qoffs, out)
         nc.sync.dma_start(offs_t[:], offs)
         nc.sync.dma_start(out=vs_raw[LAST:, :], in_=vs[0:1, :])
         for j in range(2):
-            nc.sync.dma_start(out=k_plane[j][:], in_=k_rows[:, j, :])
+            nc.sync.dma_start(out=k_raw[j][:], in_=k_rows[:, j, :])
         nc.sync.dma_start(qoffs_t[:], qoffs)
         nc.sync.dma_start(out=sink_row[LAST:, :], in_=sink.rearrange("b q o -> b (q o)"))
-        nc.sync.dma_start(out=k_raw[:], in_=k_rows[:, 2:4, :])
+        for j in range(2, 4):
+            nc.sync.dma_start(out=k_raw[j][:], in_=k_rows[:, j, :])
         for j in range(4):
             nc.sync.dma_start(out=q_raw[j][:], in_=q_rows[:, j, :])
         for h in range(2):
@@ -76,26 +74,23 @@ def tile_attend_x_router_sink_kernel(tc, xq, kT, vT, vs, sink, offs, qoffs, out)
 
         k_g = keep.tile([P, N * 4], BF16, name="k_g", align_bytes=64)
         k_places = k_g[:].rearrange("p (t s j) -> p s t j", t=4, j=4)
-        for j in range(2):
-            nc.vector.tensor_copy(k_places[:, :, :, j], k_plane[j][:].indirect(offs_t[:]))
         columns = keep.tile([P, 8], F32, name="columns")
         vs_c = columns[:, 0:4]
         sink_n = columns[:, 4:6]
         nc.scalar.activation(out=vs_c, in_=vs_ps[:, :, LAST], func=COPY)
         nc.scalar.activation(out=sink_n, in_=sink_ps[:, :, LAST], func=COPY, scale=-1.0)
-        k_pair = keep.tile([P, T, 2], BF16, name="k_pair", tag="k_pair1", align_bytes=64)
-        raw = k_raw[:].rearrange("p e n -> p n e")
-        nc.scalar.activation(out=k_pair[:, :SCALAR_TOKENS, :], in_=raw[:, :SCALAR_TOKENS, :], func=COPY)
-        nc.vector.tensor_copy(out=k_pair[:, SCALAR_TOKENS:, :], in_=raw[:, SCALAR_TOKENS:, :])
-        k_words = k_g[:].bitcast(U32).rearrange("p (t s u) -> p s t u", t=4, u=2)
-        window = k_pair[:].rearrange("p n e -> p (n e)").bitcast(U32)
-        nc.vector.tensor_copy(k_words[:, :, :, 1], window.indirect(offs_t[:]))
+        for u in range(2):
+            k_pair = keep.tile([P, 2, N], BF16, name=f"k_pair{u}")
+            for e in range(2):
+                nc.vector.tensor_copy(k_pair[:, e, :], k_raw[2 * u + e][:].indirect(offs_t[:]))
+            weave = (nc.scalar.copy, nc.vector.tensor_copy)[u]
+            weave(out=k_places[:, :, :, 2 * u : 2 * u + 2], in_=k_pair[:].rearrange("p e (s t) -> p s t e", t=4))
         k_codes = keep.tile([P, N], U32, name="k_codes", align_bytes=64)
         k_scales = keep.tile([P, N], U8, name="k_scales", align_bytes=64)
         nc.vector.quantize_mx(out=k_codes[:].bitcast(FP8X4), scales=k_scales[:], in_=k_g[:])
 
-        q_cast = keep.tile([P, 2, T], BF16, name="q_cast", tag="k_raw1", align_bytes=64)
-        q_g = keep.tile([P, NQ, 4], BF16, name="q_g", tag="k_pair1", align_bytes=64)
+        q_cast = keep.tile([P, 2, T], BF16, name="q_cast", tag="q_cast", align_bytes=64)
+        q_g = keep.tile([P, NQ, 4], BF16, name="q_g", align_bytes=64)
         for j in range(2):
             nc.scalar.activation(out=q_cast[:, j, :], in_=q_raw[j][:], func=COPY)
             nc.scalar.activation(out=q_g[:, :, j], in_=q_cast[:, j, :].indirect(qoffs_t[:]), func=COPY)
@@ -119,7 +114,7 @@ def tile_attend_x_router_sink_kernel(tc, xq, kT, vT, vs, sink, offs, qoffs, out)
             )
             scores.append(score)
 
-        v_g0 = keep.tile([P, N], BF16, name="v_g0", tag="k_raw1", align_bytes=64)
+        v_g0 = keep.tile([P, N], BF16, name="v_g0", tag="q_cast", align_bytes=64)
 
         def turn_values(h, v_g, tag):
             words = v_g[:].bitcast(F32)

@@ -60,8 +60,6 @@ def tile_attend_x_router_sink_kernel(tc, xq, kT, vT, vs, sink, offs, qoffs, out)
         placed = [keep.tile([P, T], F32, name=f"placed{h}") for h in range(2)]
         for h in range(2):
             (nc.gpsimd, nc.vector)[h].memset(placed[h][:], 0.0)
-        table = keep.tile([P, 1], F32, name="table")
-        nc.scalar.activation(out=table[:LAST, :], in_=sink_row[:LAST, 0:1], func=EXP)
 
         vs_g = keep.tile([P, N], F32, name="vs_g")
         nc.vector.tensor_copy(vs_g[:], vs_raw[:].indirect(offs_t[:]))

@@ -59,7 +59,7 @@ def tile_attend_x_router_sink_kernel(tc, xq, kT, vT, vs, sink, offs, qoffs, out)
         make_identity(nc, ident[:])
         placed = [keep.tile([P, T], F32, name=f"placed{h}") for h in range(2)]
         for h in range(2):
-            (nc.gpsimd, nc.vector)[h].memset(placed[h][:], 0.0)
+            nc.gpsimd.memset(placed[h][:], 0.0)
 
         vs_g = keep.tile([P, N], F32, name="vs_g")
         nc.vector.tensor_copy(vs_g[:], vs_raw[:].indirect(offs_t[:]))

@@ -22,6 +22,9 @@ EXP = mybir.ActivationFunctionType.Exp
 MULT = mybir.AluOpType.mult
 MIN = mybir.AluOpType.min
 
+VECTOR_SLOTS = 192
+SCALAR_TOKENS = 704
+
 
 def tile_attend_x_router_sink_kernel(tc, xq, kT, vT, vs, sink, offs, qoffs, out):
     nc = tc.nc
@@ -88,15 +91,21 @@ def tile_attend_x_router_sink_kernel(tc, xq, kT, vT, vs, sink, offs, qoffs, out)
         nc.vector.quantize_mx(out=k_codes[:].bitcast(FP8X4), scales=k_scales[:], in_=k_g[:])
 
         q_cast = keep.tile([P, 2, T], BF16, name="q_cast", tag="q_cast", align_bytes=64)
-        q_g = keep.tile([P, NQ, 4], BF16, name="q_g", align_bytes=64)
+        q_g = keep.tile([P, NQ, 4], BF16, name="q_g", tag="q_g", align_bytes=64)
         for j in range(2):
             nc.scalar.activation(out=q_cast[:, j, :], in_=q_raw[j][:], func=COPY)
-            nc.scalar.activation(out=q_g[:, :, j], in_=q_cast[:, j, :].indirect(qoffs_t[:]), func=COPY)
-        for j in range(2, 4):
-            nc.vector.tensor_copy(q_g[:, :, j], q_raw[j][:].indirect(qoffs_t[:]))
+        for c in range(2):
+            for j in range(2):
+                nc.scalar.activation(out=q_g[:, tiles[c], j], in_=q_cast[:, j, :].indirect(qoffs_t[:, lists[c]]), func=COPY)
+        nc.vector.tensor_copy(q_g[:, :, 2], q_raw[2][:].indirect(qoffs_t[:]))
+        for c in range(2):
+            nc.vector.tensor_copy(q_g[:, tiles[c], 3], q_raw[3][:].indirect(qoffs_t[:, lists[c]]))
         q_codes = keep.tile([P, NQ], U32, name="q_codes", align_bytes=64)
         q_scales = keep.tile([P, NQ], U8, name="q_scales", align_bytes=64)
-        nc.vector.quantize_mx(out=q_codes[:].bitcast(FP8X4), scales=q_scales[:], in_=q_g[:].rearrange("p q j -> p (q j)"))
+        for cols in tiles:
+            nc.vector.quantize_mx(
+                out=q_codes[:, cols].bitcast(FP8X4), scales=q_scales[:, cols], in_=q_g[:, cols, :].rearrange("p q j -> p (q j)")
+            )
 
         scores = []
         for c in range(2):
@@ -112,7 +121,7 @@ def tile_attend_x_router_sink_kernel(tc, xq, kT, vT, vs, sink, offs, qoffs, out)
             )
             scores.append(score)
 
-        v_g0 = keep.tile([P, N], BF16, name="v_g0", tag="q_cast", align_bytes=64)
+        v_g0 = keep.tile([P, N], BF16, name="v_g0", tag="q_g", align_bytes=64)
 
         def turn_values(h, v_g, tag):
             words = v_g[:].bitcast(F32)
@@ -134,10 +143,11 @@ def tile_attend_x_router_sink_kernel(tc, xq, kT, vT, vs, sink, offs, qoffs, out)
             nc.vector.quantize_mx(out=codes[:].bitcast(FP8X4), scales=scales[:], in_=v_s[:])
             return codes, scales
 
-        v_cast = keep.tile([P, T], BF16, name="v_cast", tag="v_cast", align_bytes=64)
-        nc.scalar.activation(out=v_cast[:], in_=v_raw[0][:], func=COPY)
-        nc.vector.tensor_copy(v_g0[:, : N // 2], v_raw[0][:].indirect(offs_t[:, : N // 32]))
-        nc.scalar.activation(out=v_g0[:, N // 2 :], in_=v_cast[:].indirect(offs_t[:, N // 32 :]), func=COPY)
+        v_cast = keep.tile([P, T], BF16, name="v_cast", tag="q_cast", align_bytes=64)
+        nc.scalar.activation(out=v_cast[:, :SCALAR_TOKENS], in_=v_raw[0][:, :SCALAR_TOKENS], func=COPY)
+        nc.vector.tensor_copy(out=v_cast[:, SCALAR_TOKENS:], in_=v_raw[0][:, SCALAR_TOKENS:])
+        nc.vector.tensor_copy(v_g0[:, :VECTOR_SLOTS], v_raw[0][:].indirect(offs_t[:, : VECTOR_SLOTS // 16]))
+        nc.scalar.activation(out=v_g0[:, VECTOR_SLOTS:], in_=v_cast[:].indirect(offs_t[:, VECTOR_SLOTS // 16 :]), func=COPY)
         v_ps0 = turn_values(0, v_g0, "value")
 
         neg_max = []
@@ -154,7 +164,7 @@ def tile_attend_x_router_sink_kernel(tc, xq, kT, vT, vs, sink, offs, qoffs, out)
                 accum_out=least[:],
             )
             neg_max.append(least)
-        v_g1 = keep.tile([P, N], BF16, name="v_g1", tag="v_cast", align_bytes=64)
+        v_g1 = keep.tile([P, N], BF16, name="v_g1", tag="q_cast", align_bytes=64)
         nc.vector.tensor_copy(v_g1[:], v_raw[1][:].indirect(offs_t[:]))
         terms = keep.tile([P, 2, 3], F32, name="terms")
         summed = keep.tile([P, 2, 3], F32, name="summed")

@@ -23,7 +23,7 @@ MULT = mybir.AluOpType.mult
 MIN = mybir.AluOpType.min
 
 VECTOR_SLOTS = 192
-SCALAR_TOKENS = 704
+SCALAR_TOKENS = 512
 
 
 def tile_attend_x_router_sink_kernel(tc, xq, kT, vT, vs, sink, offs, qoffs, out):

@@ -45,14 +45,14 @@ def tile_attend_x_router_sink_kernel(tc, xq, kT, vT, vs, sink, offs, qoffs, out)
         q_raw = [keep.tile([P, T], F32, name=f"q_raw{j}") for j in range(4)]
         k_rows = kT.rearrange("(p j) n -> p j n", j=4)
         q_rows = xq.rearrange("(p j) n -> p j n", j=4)
+        nc.scalar.dma_start(out=vs_raw[LAST:, :], in_=vs[0:1, :])
+        nc.scalar.dma_start(out=sink_row[LAST:, :], in_=sink.rearrange("b q o -> b (q o)"))
+        nc.sync.dma_start(out=k_raw[0][:], in_=k_rows[:, 0, :])
         nc.sync.dma_start(offs_t[:], offs)
-        nc.sync.dma_start(out=vs_raw[LAST:, :], in_=vs[0:1, :])
-        for j in range(2):
+        for j in range(1, 3):
             nc.sync.dma_start(out=k_raw[j][:], in_=k_rows[:, j, :])
         nc.sync.dma_start(qoffs_t[:], qoffs)
-        nc.sync.dma_start(out=sink_row[LAST:, :], in_=sink.rearrange("b q o -> b (q o)"))
-        for j in range(2, 4):
-            nc.sync.dma_start(out=k_raw[j][:], in_=k_rows[:, j, :])
+        nc.sync.dma_start(out=k_raw[3][:], in_=k_rows[:, 3, :])
         for j in range(4):
             nc.sync.dma_start(out=q_raw[j][:], in_=q_rows[:, j, :])
         for h in range(2):
@@ -83,7 +83,12 @@ def tile_attend_x_router_sink_kernel(tc, xq, kT, vT, vs, sink, offs, qoffs, out)
         for u in range(2):
             k_pair = keep.tile([P, 2, N], BF16, name=f"k_pair{u}")
             for e in range(2):
-                nc.vector.tensor_copy(k_pair[:, e, :], k_raw[2 * u + e][:].indirect(offs_t[:]))
+                if u == e == 0:
+                    k_cast = keep.tile([P, T], BF16, name="k_cast")
+                    nc.scalar.activation(out=k_cast[:], in_=k_raw[0][:], func=COPY)
+                    nc.scalar.activation(out=k_pair[:, 0, :], in_=k_cast[:].indirect(offs_t[:]), func=COPY)
+                else:
+                    nc.vector.tensor_copy(k_pair[:, e, :], k_raw[2 * u + e][:].indirect(offs_t[:]))
             weave = (nc.scalar.copy, nc.vector.tensor_copy)[u]
             weave(out=k_places[:, :, :, 2 * u : 2 * u + 2], in_=k_pair[:].rearrange("p e (s t) -> p s t e", t=4))
         k_codes = keep.tile([P, N], U32, name="k_codes", align_bytes=64)

@@ -75,11 +75,12 @@ def tile_attend_x_router_sink_kernel(tc, xq, kT, vT, vs, sink, offs, qoffs, out)
 
         k_g = keep.tile([P, N * 4], BF16, name="k_g", align_bytes=64)
         k_places = k_g[:].rearrange("p (t s j) -> p s t j", t=4, j=4)
-        columns = keep.tile([P, 8], F32, name="columns")
-        vs_c = columns[:, 0:4]
-        sink_n = columns[:, 4:6]
-        nc.scalar.activation(out=vs_c, in_=vs_ps[:, :, LAST], func=COPY)
-        nc.scalar.activation(out=sink_n, in_=sink_ps[:, :, LAST], func=COPY, scale=-1.0)
+        sink_n = keep.tile([P, 2], F32, name="sink_n")
+        vs_c = [keep.tile([P, 4], F32, name=f"vs_c{c}", tag=f"vs_c{c}", align_bytes=64) for c in range(3)]
+        nc.scalar.activation(out=vs_c[2][:], in_=vs_ps[:, :, LAST], func=COPY)
+        for c in range(2):
+            nc.gpsimd.tensor_copy(vs_c[c][:], vs_c[2][:])
+        nc.scalar.activation(out=sink_n[:], in_=sink_ps[:, :, LAST], func=COPY, scale=-1.0)
         for u in range(2):
             k_pair = keep.tile([P, 2, N], BF16, name=f"k_pair{u}")
             for e in range(2):
@@ -205,13 +206,15 @@ def tile_attend_x_router_sink_kernel(tc, xq, kT, vT, vs, sink, offs, qoffs, out)
         w_scales = keep.tile([P, NQ], U8, name="w_scales", align_bytes=64)
 
         def weigh(c):
-            w_s = keep.tile([P, P, 4], BF16, name=f"w_s{c}", align_bytes=64)
-            nc.vector.tensor_tensor(
-                out=w_s[:],
-                in0=p_banks[c][:].rearrange("s t q -> s q t"),
-                in1=vs_c.unsqueeze(1).to_broadcast([P, P, 4]),
-                op=MULT,
-            )
+            w_s = keep.tile([P, P, 4], BF16, name=f"w_s{c}", tag=("w_s0", "vs_c0")[c], align_bytes=64)
+            parts = ([(slice(0, P), vs_c[0])], [(slice(0, P // 2), vs_c[1]), (slice(P // 2, P), vs_c[2])])[c]
+            for queries, scales in parts:
+                nc.vector.tensor_tensor(
+                    out=w_s[:, queries, :],
+                    in0=p_banks[c][:].rearrange("s t q -> s q t")[:, queries, :],
+                    in1=scales[:].unsqueeze(1).to_broadcast([P, queries.stop - queries.start, 4]),
+                    op=MULT,
+                )
             return w_s
 
         def quantise_weights(c, w_s):
@@ -240,7 +243,7 @@ def tile_attend_x_router_sink_kernel(tc, xq, kT, vT, vs, sink, offs, qoffs, out)
                 start=True,
                 stop=True,
             )
-            y = keep.tile([P, width], F32, name=f"y_{tag}")
+            y = keep.tile([P, width], F32, name=f"y_{tag}", tag={"y0": "vs_c1"}.get(tag, f"y_{tag}"), align_bytes=64)
             nc.scalar.activation(out=y[:], in_=y_ps[:], func=COPY)
             return y
 

@@ -77,9 +77,8 @@ def tile_attend_x_router_sink_kernel(tc, xq, kT, vT, vs, sink, offs, qoffs, out)
         k_places = k_g[:].rearrange("p (t s j) -> p s t j", t=4, j=4)
         sink_n = keep.tile([P, 2], F32, name="sink_n")
         vs_c = [keep.tile([P, 4], F32, name=f"vs_c{c}", tag=f"vs_c{c}", align_bytes=64) for c in range(3)]
-        nc.scalar.activation(out=vs_c[2][:], in_=vs_ps[:, :, LAST], func=COPY)
-        for c in range(2):
-            nc.gpsimd.tensor_copy(vs_c[c][:], vs_c[2][:])
+        for c in range(3):
+            nc.scalar.activation(out=vs_c[c][:], in_=vs_ps[:, :, LAST], func=COPY)
         nc.scalar.activation(out=sink_n[:], in_=sink_ps[:, :, LAST], func=COPY, scale=-1.0)
         for u in range(2):
             k_pair = keep.tile([P, 2, N], BF16, name=f"k_pair{u}")
@@ -133,18 +132,18 @@ def tile_attend_x_router_sink_kernel(tc, xq, kT, vT, vs, sink, offs, qoffs, out)
             words = v_g[:].bitcast(F32)
             v_ps = psum.tile([P, 2, P], F32, name=f"v_ps{h}", tag=tag)
             for u in range(2):
-                nc.tensor.transpose(v_ps[:, u, :], words[:, u::2], ident[:])
+                nc.tensor.transpose(v_ps[:, u, :], (words[:, u::2], words[:, tiles[u]])[h], ident[:])
             return v_ps
 
         def interleave_values(h, v_ps):
-            v_s = keep.tile([P, N], BF16, name=f"v_s{h}", tag=f"neg_max{h}", align_bytes=64)
+            v_s = keep.tile([P, N], BF16, name=f"v_s{h}", tag=("neg_max1", "v_s1")[h], align_bytes=64)
             nc.scalar.copy(
                 out=v_s[:].bitcast(F32).rearrange("s (e u) -> s e u", u=2), in_=v_ps[:].rearrange("s u e -> s e u")
             )
             return v_s
 
         def quantise_values(h, v_s):
-            codes = keep.tile([P, P], U32, name=f"v_codes{h}", align_bytes=64)
+            codes = keep.tile([P, P], U32, name=f"v_codes{h}", tag=("v_codes0", "p11")[h], align_bytes=64)
             scales = keep.tile([P, P], U8, name=f"v_scales{h}", align_bytes=64)
             nc.vector.quantize_mx(out=codes[:].bitcast(FP8X4), scales=scales[:], in_=v_s[:])
             return codes, scales
@@ -171,34 +170,34 @@ def tile_attend_x_router_sink_kernel(tc, xq, kT, vT, vs, sink, offs, qoffs, out)
             )
             neg_max.append(least)
         v_g1 = keep.tile([P, N], BF16, name="v_g1", tag="q_cast", align_bytes=64)
-        nc.vector.tensor_copy(v_g1[:], v_raw[1][:].indirect(offs_t[:]))
+        nc.vector.tensor_copy(v_g1[:].rearrange("p (u s e) -> p s u e", u=2, e=2), v_raw[1][:].indirect(offs_t[:]))
         terms = keep.tile([P, 2, 3], F32, name="terms")
         summed = keep.tile([P, 2, 3], F32, name="summed")
         totals = keep.tile([P, 2], F32, name="totals")
         p_banks = []
         for c in range(2):
-            p = keep.tile([P, 4, P], F32, name=f"p{c}", tag=f"p_sb{c}")
             p_ps = psum.tile([P, 4, P], F32, name=f"p_ps{c}", tag=f"p{c}")
             dealt = scores[c][:].rearrange("q (t s) -> q t s", t=4)
             for half in range(2):
                 places = slice(2 * half, 2 * half + 2)
+                p = keep.tile([P, 2, P], F32, name=f"p{c}{half}", tag=f"p{c}{half}", align_bytes=64)
                 nc.scalar.activation(
-                    out=p[:, places, :],
+                    out=p[:],
                     in_=dealt[:, places, :],
                     func=EXP,
                     bias=neg_max[c][:],
                     scale=1.0,
                     accum_out=terms[:, c, half : half + 1],
                 )
-                for t in (2 * half, 2 * half + 1):
-                    nc.tensor.transpose(p_ps[:, t, :], p[:, t, :], ident[:])
+                for t in range(2):
+                    nc.tensor.transpose(p_ps[:, 2 * half + t, :], p[:, t, :], ident[:])
                 if half == 0:
                     nc.scalar.activation(
                         out=terms[:, c, 2:3], in_=sink_n[:, c : c + 1], func=EXP, bias=neg_max[c][:], scale=-1.0
                     )
-            nc.scalar.activation(out=summed[:, c, :], in_=terms[:, c, :], func=IDENTITY, accum_out=totals[:, c : c + 1])
-            if c == 0:
+            if c == 1:
                 v_s0 = interleave_values(0, v_ps0)
+            nc.scalar.activation(out=summed[:, c, :], in_=terms[:, c, :], func=IDENTITY, accum_out=totals[:, c : c + 1])
             p_banks.append(p_ps)
         v_ps1 = turn_values(1, v_g1, "score1")
 
@@ -225,7 +224,7 @@ def tile_attend_x_router_sink_kernel(tc, xq, kT, vT, vs, sink, offs, qoffs, out)
         recip_b = keep.tile([P, NQ], F32, name="recip_b")
 
         def spread_reciprocals(c):
-            recip = keep.tile([P, 1], F32, name=f"recip{c}", tag=("recip0", "p_sb1")[c])
+            recip = keep.tile([P, 1], F32, name=f"recip{c}", tag=("p01", "p10")[c], align_bytes=64)
             nc.vector.reciprocal(out=recip[:], in_=totals[:, c : c + 1])
             r_ps = psum.tile([P, P], F32, name=f"r_ps{c}", tag=("row", "value")[c])
             nc.tensor.transpose(r_ps[:], recip[:].to_broadcast([P, P]), ident[:])
@@ -243,24 +242,26 @@ def tile_attend_x_router_sink_kernel(tc, xq, kT, vT, vs, sink, offs, qoffs, out)
                 start=True,
                 stop=True,
             )
-            y = keep.tile([P, width], F32, name=f"y_{tag}", tag={"y0": "vs_c1"}.get(tag, f"y_{tag}"), align_bytes=64)
-            nc.scalar.activation(out=y[:], in_=y_ps[:], func=COPY)
+            y_tile = keep.tile([P, width], F32, name=f"y_{tag}", tag={"y0": "vs_c1"}.get(tag, f"y_{tag}"), align_bytes=64)
+            y = y_tile[:]
+            nc.scalar.activation(out=y, in_=y_ps[:], func=COPY)
             return y
 
         def place(h, y, cols, entries):
-            nc.vector.tensor_tensor(placed[h][:].indirect(qoffs_t[:, entries]), y[:], recip_b[:, cols], MULT)
+            nc.vector.tensor_tensor(placed[h][:].indirect(qoffs_t[:, entries]), y, recip_b[:, cols], MULT)
 
-        spread_reciprocals(0)
         w_s0 = weigh(0)
+        spread_reciprocals(0)
         v_mx0 = quantise_values(0, v_s0)
         quantise_weights(0, w_s0)
+        v_s1 = interleave_values(1, v_ps1)
         y_first = multiply(v_mx0, tiles[0], "y0")
         w_s1 = weigh(1)
         spread_reciprocals(1)
+        v_mx1 = quantise_values(1, v_s1)
         quantise_weights(1, w_s1)
         y_second = multiply(v_mx0, tiles[1], "y1")
         place(0, y_first, tiles[0], lists[0])
-        v_mx1 = quantise_values(1, interleave_values(1, v_ps1))
         place(0, y_second, tiles[1], lists[1])
         nc.sync.dma_start(out=out[tiles[0], :], in_=placed[0][:])
         place(1, multiply(v_mx1, slice(0, NQ), "score0"), slice(0, NQ), slice(0, NQ // 16))

@@ -17,10 +17,11 @@ U8 = mybir.dt.uint8
 FP8X4 = mybir.dt.float8_e4m3fn_x4
 
 COPY = mybir.ActivationFunctionType.Copy
-IDENTITY = mybir.ActivationFunctionType.Identity
 EXP = mybir.ActivationFunctionType.Exp
+ADD = mybir.AluOpType.add
 MULT = mybir.AluOpType.mult
 MIN = mybir.AluOpType.min
+POW = mybir.AluOpType.pow
 
 VECTOR_SLOTS = 192
 SCALAR_TOKENS = 512
@@ -60,6 +61,8 @@ def tile_attend_x_router_sink_kernel(tc, xq, kT, vT, vs, sink, offs, qoffs, out)
 
         ident = keep.tile([P, P], F32, name="ident")
         make_identity(nc, ident[:])
+        minus_one = keep.tile([P, 1], F32, name="minus_one")
+        nc.gpsimd.memset(minus_one[:], -1.0)
         placed = [keep.tile([P, T], F32, name=f"placed{h}") for h in range(2)]
         for h in range(2):
             nc.gpsimd.memset(placed[h][:], 0.0)
@@ -130,7 +133,7 @@ def tile_attend_x_router_sink_kernel(tc, xq, kT, vT, vs, sink, offs, qoffs, out)
 
         def turn_values(h, v_g, tag):
             words = v_g[:].bitcast(F32)
-            v_ps = psum.tile([P, 2, P], F32, name=f"v_ps{h}", tag=tag)
+            v_ps = psum.tile([P, 3, P], F32, name=f"v_ps{h}", tag=tag)
             for u in range(2):
                 nc.tensor.transpose(v_ps[:, u, :], (words[:, u::2], words[:, tiles[u]])[h], ident[:])
             return v_ps
@@ -138,7 +141,7 @@ def tile_attend_x_router_sink_kernel(tc, xq, kT, vT, vs, sink, offs, qoffs, out)
         def interleave_values(h, v_ps):
             v_s = keep.tile([P, N], BF16, name=f"v_s{h}", tag=("neg_max1", "v_s1")[h], align_bytes=64)
             nc.scalar.copy(
-                out=v_s[:].bitcast(F32).rearrange("s (e u) -> s e u", u=2), in_=v_ps[:].rearrange("s u e -> s e u")
+                out=v_s[:].bitcast(F32).rearrange("s (e u) -> s e u", u=2), in_=v_ps[:, :2, :].rearrange("s u e -> s e u")
             )
             return v_s
 
@@ -171,8 +174,7 @@ def tile_attend_x_router_sink_kernel(tc, xq, kT, vT, vs, sink, offs, qoffs, out)
             neg_max.append(least)
         v_g1 = keep.tile([P, N], BF16, name="v_g1", tag="q_cast", align_bytes=64)
         nc.vector.tensor_copy(v_g1[:].rearrange("p (u s e) -> p s u e", u=2, e=2), v_raw[1][:].indirect(offs_t[:]))
-        terms = keep.tile([P, 2, 3], F32, name="terms")
-        summed = keep.tile([P, 2, 3], F32, name="summed")
+        terms = keep.tile([P, 2, 3], F32, name="terms", tag="terms")
         totals = keep.tile([P, 2], F32, name="totals")
         p_banks = []
         for c in range(2):
@@ -197,7 +199,14 @@ def tile_attend_x_router_sink_kernel(tc, xq, kT, vT, vs, sink, offs, qoffs, out)
                     )
             if c == 1:
                 v_s0 = interleave_values(0, v_ps0)
-            nc.scalar.activation(out=summed[:, c, :], in_=terms[:, c, :], func=IDENTITY, accum_out=totals[:, c : c + 1])
+            nc.gpsimd.tensor_scalar(
+                out=totals[:, c : c + 1],
+                in0=terms[:, c, 0:1],
+                scalar1=terms[:, c, 1:2],
+                scalar2=terms[:, c, 2:3],
+                op0=ADD,
+                op1=ADD,
+            )
             p_banks.append(p_ps)
         v_ps1 = turn_values(1, v_g1, "score1")
 
@@ -221,14 +230,21 @@ def tile_attend_x_router_sink_kernel(tc, xq, kT, vT, vs, sink, offs, qoffs, out)
                 out=w_codes[:, tiles[c]].bitcast(FP8X4), scales=w_scales[:, tiles[c]], in_=w_s[:].rearrange("s q t -> s (q t)")
             )
 
-        recip_b = keep.tile([P, NQ], F32, name="recip_b")
+        recip_b = keep.tile([P, NQ], F32, name="recip_b", tag="terms")
 
         def spread_reciprocals(c):
-            recip = keep.tile([P, 1], F32, name=f"recip{c}", tag=("p01", "p10")[c], align_bytes=64)
-            nc.vector.reciprocal(out=recip[:], in_=totals[:, c : c + 1])
-            r_ps = psum.tile([P, P], F32, name=f"r_ps{c}", tag=("row", "value")[c])
-            nc.tensor.transpose(r_ps[:], recip[:].to_broadcast([P, P]), ident[:])
-            nc.scalar.activation(out=recip_b[:, tiles[c]], in_=r_ps[:], func=COPY)
+            recip = keep.tile([P, 1], F32, name=f"recip{c}", tag=("recip0", "w_s0")[c], align_bytes=64)
+            nc.gpsimd.tensor_tensor(out=recip[:], in0=totals[:, c : c + 1], in1=minus_one[:], op=POW)
+            if c == 0:
+                r_ps = v_ps1[:, 2, :]
+            else:
+                r_bank = psum.tile([P, P], F32, name="r_bank", tag="row")
+                r_ps = r_bank[:]
+            nc.tensor.transpose(r_ps, recip[:].to_broadcast([P, P]), ident[:])
+            return r_ps
+
+        def copy_reciprocals(c, r_ps):
+            nc.scalar.activation(out=recip_b[:, tiles[c]], in_=r_ps, func=COPY)
 
         def multiply(v_mx, cols, tag):
             width = cols.stop - cols.start
@@ -251,13 +267,14 @@ def tile_attend_x_router_sink_kernel(tc, xq, kT, vT, vs, sink, offs, qoffs, out)
             nc.vector.tensor_tensor(placed[h][:].indirect(qoffs_t[:, entries]), y, recip_b[:, cols], MULT)
 
         w_s0 = weigh(0)
-        spread_reciprocals(0)
+        r_ps0 = spread_reciprocals(0)
         v_mx0 = quantise_values(0, v_s0)
         quantise_weights(0, w_s0)
         v_s1 = interleave_values(1, v_ps1)
+        copy_reciprocals(0, r_ps0)
         y_first = multiply(v_mx0, tiles[0], "y0")
         w_s1 = weigh(1)
-        spread_reciprocals(1)
+        copy_reciprocals(1, spread_reciprocals(1))
         v_mx1 = quantise_values(1, v_s1)
         quantise_weights(1, w_s1)
         y_second = multiply(v_mx0, tiles[1], "y1")

@@ -77,23 +77,25 @@ def tile_attend_x_router_sink_kernel(tc, xq, kT, vT, vs, sink, offs, qoffs, out)
             nc.tensor.transpose(sink_ps[:, c, :], sink_row[:, tiles[c]], ident[:])
 
         k_g = keep.tile([P, N * 4], BF16, name="k_g", align_bytes=64)
-        k_places = k_g[:].rearrange("p (t s j) -> p s t j", t=4, j=4)
         sink_n = keep.tile([P, 2], F32, name="sink_n")
-        vs_c = [keep.tile([P, 4], F32, name=f"vs_c{c}", tag=f"vs_c{c}", align_bytes=64) for c in range(3)]
-        for c in range(3):
+        vs_c = [keep.tile([P, 4], F32, name=f"vs_c{c}", tag=f"vs_c{c}", align_bytes=64) for c in range(2)]
+        for c in range(2):
             nc.scalar.activation(out=vs_c[c][:], in_=vs_ps[:, :, LAST], func=COPY)
         nc.scalar.activation(out=sink_n[:], in_=sink_ps[:, :, LAST], func=COPY, scale=-1.0)
-        for u in range(2):
-            k_pair = keep.tile([P, 2, N], BF16, name=f"k_pair{u}")
-            for e in range(2):
-                if u == e == 0:
-                    k_cast = keep.tile([P, T], BF16, name="k_cast")
-                    nc.scalar.activation(out=k_cast[:], in_=k_raw[0][:], func=COPY)
-                    nc.scalar.activation(out=k_pair[:, 0, :], in_=k_cast[:].indirect(offs_t[:]), func=COPY)
-                else:
-                    nc.vector.tensor_copy(k_pair[:, e, :], k_raw[2 * u + e][:].indirect(offs_t[:]))
-            weave = (nc.scalar.copy, nc.vector.tensor_copy)[u]
-            weave(out=k_places[:, :, :, 2 * u : 2 * u + 2], in_=k_pair[:].rearrange("p e (s t) -> p s t e", t=4))
+        k_planes = keep.tile([P, 2, N], BF16, name="k_planes")
+        k_pairs = keep.tile([P, 4 * N], BF16, name="k_pairs")
+        pair_places = k_pairs[:].rearrange("p (u t s e) -> p u s t e", u=2, t=4, e=2)
+        k_cast = keep.tile([P, T], BF16, name="k_cast")
+        nc.scalar.activation(out=k_cast[:], in_=k_raw[0][:], func=COPY)
+        nc.scalar.activation(out=k_planes[:, 0, :], in_=k_cast[:].indirect(offs_t[:]), func=COPY)
+        nc.vector.tensor_copy(k_planes[:, 1, :], k_raw[1][:].indirect(offs_t[:]))
+        nc.scalar.copy(out=pair_places[:, 0], in_=k_planes[:].rearrange("p e (s t) -> p s t e", t=4))
+        for e in range(2):
+            nc.vector.tensor_copy(pair_places[:, 1, :, :, e], k_raw[2 + e][:].indirect(offs_t[:]))
+        nc.vector.tensor_copy(
+            out=k_g[:].bitcast(F32).rearrange("p (n u) -> p n u", u=2),
+            in_=k_pairs[:].bitcast(F32).rearrange("p (u n) -> p n u", u=2),
+        )
         k_codes = keep.tile([P, N], U32, name="k_codes", align_bytes=64)
         k_scales = keep.tile([P, N], U8, name="k_scales", align_bytes=64)
         nc.vector.quantize_mx(out=k_codes[:].bitcast(FP8X4), scales=k_scales[:], in_=k_g[:])
@@ -193,7 +195,7 @@ def tile_attend_x_router_sink_kernel(tc, xq, kT, vT, vs, sink, offs, qoffs, out)
                 )
                 for t in range(2):
                     nc.tensor.transpose(p_ps[:, 2 * half + t, :], p[:, t, :], ident[:])
-                if half == 0:
+                if half == 1:
                     nc.scalar.activation(
                         out=terms[:, c, 2:3], in_=sink_n[:, c : c + 1], func=EXP, bias=neg_max[c][:], scale=-1.0
                     )
@@ -215,14 +217,12 @@ def tile_attend_x_router_sink_kernel(tc, xq, kT, vT, vs, sink, offs, qoffs, out)
 
         def weigh(c):
             w_s = keep.tile([P, P, 4], BF16, name=f"w_s{c}", tag=("w_s0", "vs_c0")[c], align_bytes=64)
-            parts = ([(slice(0, P), vs_c[0])], [(slice(0, P // 2), vs_c[1]), (slice(P // 2, P), vs_c[2])])[c]
-            for queries, scales in parts:
-                nc.vector.tensor_tensor(
-                    out=w_s[:, queries, :],
-                    in0=p_banks[c][:].rearrange("s t q -> s q t")[:, queries, :],
-                    in1=scales[:].unsqueeze(1).to_broadcast([P, queries.stop - queries.start, 4]),
-                    op=MULT,
-                )
+            nc.vector.tensor_tensor(
+                out=w_s[:],
+                in0=p_banks[c][:].rearrange("s t q -> s q t"),
+                in1=vs_c[c][:].unsqueeze(1).to_broadcast([P, P, 4]),
+                op=MULT,
+            )
             return w_s
 
         def quantise_weights(c, w_s):
@@ -258,8 +258,11 @@ def tile_attend_x_router_sink_kernel(tc, xq, kT, vT, vs, sink, offs, qoffs, out)
                 start=True,
                 stop=True,
             )
-            y_tile = keep.tile([P, width], F32, name=f"y_{tag}", tag={"y0": "vs_c1"}.get(tag, f"y_{tag}"), align_bytes=64)
-            y = y_tile[:]
+            if tag == "y0":
+                y = v_g1[:].bitcast(F32)[:, :P]
+            else:
+                y_tile = keep.tile([P, width], F32, name=f"y_{tag}")
+                y = y_tile[:]
             nc.scalar.activation(out=y, in_=y_ps[:], func=COPY)
             return y
 

@@ -18,6 +18,7 @@ FP8X4 = mybir.dt.float8_e4m3fn_x4
 
 COPY = mybir.ActivationFunctionType.Copy
 EXP = mybir.ActivationFunctionType.Exp
+IDENTITY = mybir.ActivationFunctionType.Identity
 ADD = mybir.AluOpType.add
 MULT = mybir.AluOpType.mult
 MIN = mybir.AluOpType.min
@@ -178,6 +179,7 @@ def tile_attend_x_router_sink_kernel(tc, xq, kT, vT, vs, sink, offs, qoffs, out)
         nc.vector.tensor_copy(v_g1[:].rearrange("p (u s e) -> p s u e", u=2, e=2), v_raw[1][:].indirect(offs_t[:]))
         terms = keep.tile([P, 2, 3], F32, name="terms", tag="terms")
         totals = keep.tile([P, 2], F32, name="totals")
+        passed = keep.tile([P, 3], F32, name="passed")
         p_banks = []
         for c in range(2):
             p_ps = psum.tile([P, 4, P], F32, name=f"p_ps{c}", tag=f"p{c}")
@@ -201,14 +203,16 @@ def tile_attend_x_router_sink_kernel(tc, xq, kT, vT, vs, sink, offs, qoffs, out)
                     )
             if c == 1:
                 v_s0 = interleave_values(0, v_ps0)
-            nc.gpsimd.tensor_scalar(
-                out=totals[:, c : c + 1],
-                in0=terms[:, c, 0:1],
-                scalar1=terms[:, c, 1:2],
-                scalar2=terms[:, c, 2:3],
-                op0=ADD,
-                op1=ADD,
-            )
+                nc.scalar.activation(out=passed[:], in_=terms[:, c, :], func=IDENTITY, accum_out=totals[:, c : c + 1])
+            else:
+                nc.gpsimd.tensor_scalar(
+                    out=totals[:, c : c + 1],
+                    in0=terms[:, c, 0:1],
+                    scalar1=terms[:, c, 1:2],
+                    scalar2=terms[:, c, 2:3],
+                    op0=ADD,
+                    op1=ADD,
+                )
             p_banks.append(p_ps)
         v_ps1 = turn_values(1, v_g1, "score1")
 
@@ -234,7 +238,10 @@ def tile_attend_x_router_sink_kernel(tc, xq, kT, vT, vs, sink, offs, qoffs, out)
 
         def spread_reciprocals(c):
             recip = keep.tile([P, 1], F32, name=f"recip{c}", tag=("recip0", "w_s0")[c], align_bytes=64)
-            nc.gpsimd.tensor_tensor(out=recip[:], in0=totals[:, c : c + 1], in1=minus_one[:], op=POW)
+            if c == 0:
+                nc.gpsimd.tensor_tensor(out=recip[:], in0=totals[:, c : c + 1], in1=minus_one[:], op=POW)
+            else:
+                nc.vector.reciprocal(out=recip[:], in_=totals[:, c : c + 1])
             if c == 0:
                 r_ps = v_ps1[:, 2, :]
             else:

@@ -20,11 +20,11 @@ COPY = mybir.ActivationFunctionType.Copy
 EXP = mybir.ActivationFunctionType.Exp
 IDENTITY = mybir.ActivationFunctionType.Identity
 ADD = mybir.AluOpType.add
+POW = mybir.AluOpType.pow
 MULT = mybir.AluOpType.mult
 MIN = mybir.AluOpType.min
-POW = mybir.AluOpType.pow
 
-VECTOR_SLOTS = 192
+VECTOR_SLOTS = 128
 SCALAR_TOKENS = 512
 
 
@@ -78,11 +78,12 @@ def tile_attend_x_router_sink_kernel(tc, xq, kT, vT, vs, sink, offs, qoffs, out)
             nc.tensor.transpose(sink_ps[:, c, :], sink_row[:, tiles[c]], ident[:])
 
         k_g = keep.tile([P, N * 4], BF16, name="k_g", align_bytes=64)
-        sink_n = keep.tile([P, 2], F32, name="sink_n")
+        flipped = keep.tile([P, 2, N + 16], F32, name="flipped", align_bytes=64)
+        sink_n = flipped[:, :, N]
         vs_c = [keep.tile([P, 4], F32, name=f"vs_c{c}", tag=f"vs_c{c}", align_bytes=64) for c in range(2)]
         for c in range(2):
             nc.scalar.activation(out=vs_c[c][:], in_=vs_ps[:, :, LAST], func=COPY)
-        nc.scalar.activation(out=sink_n[:], in_=sink_ps[:, :, LAST], func=COPY, scale=-1.0)
+        nc.scalar.activation(out=sink_n, in_=sink_ps[:, :, LAST], func=COPY, scale=-1.0)
         k_planes = keep.tile([P, 2, N], BF16, name="k_planes")
         k_pairs = keep.tile([P, 4 * N], BF16, name="k_pairs")
         pair_places = k_pairs[:].rearrange("p (u t s e) -> p u s t e", u=2, t=4, e=2)
@@ -138,15 +139,15 @@ def tile_attend_x_router_sink_kernel(tc, xq, kT, vT, vs, sink, offs, qoffs, out)
             words = v_g[:].bitcast(F32)
             v_ps = psum.tile([P, 3, P], F32, name=f"v_ps{h}", tag=tag)
             for u in range(2):
-                nc.tensor.transpose(v_ps[:, u, :], (words[:, u::2], words[:, tiles[u]])[h], ident[:])
+                nc.tensor.transpose(v_ps[:, u, :], words[:, tiles[u]], ident[:])
             return v_ps
 
+        second_values = keep.tile([P, N // 2], F32, name="second_values", align_bytes=64)
+
         def interleave_values(h, v_ps):
-            v_s = keep.tile([P, N], BF16, name=f"v_s{h}", tag=("neg_max1", "v_s1")[h], align_bytes=64)
-            nc.scalar.copy(
-                out=v_s[:].bitcast(F32).rearrange("s (e u) -> s e u", u=2), in_=v_ps[:, :2, :].rearrange("s u e -> s e u")
-            )
-            return v_s
+            words = (flipped[:, 1, N // 2 : N], second_values[:])[h]
+            nc.scalar.copy(out=words.rearrange("s (e u) -> s e u", u=2), in_=v_ps[:, :2, :].rearrange("s u e -> s e u"))
+            return words.bitcast(BF16)
 
         def quantise_values(h, v_s):
             codes = keep.tile([P, P], U32, name=f"v_codes{h}", tag=("v_codes0", "p11")[h], align_bytes=64)
@@ -157,63 +158,49 @@ def tile_attend_x_router_sink_kernel(tc, xq, kT, vT, vs, sink, offs, qoffs, out)
         v_cast = keep.tile([P, T], BF16, name="v_cast", tag="q_cast", align_bytes=64)
         nc.scalar.activation(out=v_cast[:, :SCALAR_TOKENS], in_=v_raw[0][:, :SCALAR_TOKENS], func=COPY)
         nc.vector.tensor_copy(out=v_cast[:, SCALAR_TOKENS:], in_=v_raw[0][:, SCALAR_TOKENS:])
-        nc.vector.tensor_copy(v_g0[:, :VECTOR_SLOTS], v_raw[0][:].indirect(offs_t[:, : VECTOR_SLOTS // 16]))
-        nc.scalar.activation(out=v_g0[:, VECTOR_SLOTS:], in_=v_cast[:].indirect(offs_t[:, VECTOR_SLOTS // 16 :]), func=COPY)
+        v0_places = v_g0[:].rearrange("p (u s e) -> p s u e", u=2, e=2)
+        nc.vector.tensor_copy(v0_places[:, : VECTOR_SLOTS // 4], v_raw[0][:].indirect(offs_t[:, : VECTOR_SLOTS // 16]))
+        nc.scalar.activation(
+            out=v0_places[:, VECTOR_SLOTS // 4 :], in_=v_cast[:].indirect(offs_t[:, VECTOR_SLOTS // 16 :]), func=COPY
+        )
         v_ps0 = turn_values(0, v_g0, "value")
 
-        neg_max = []
-        flipped = keep.tile([P, 2, N], F32, name="flipped", tag="v_raw0", align_bytes=64)
+        neg_max = keep.tile([P, 2], F32, name="neg_max", tag="v_raw0", align_bytes=64)
         for c in range(2):
-            least = keep.tile([P, 1], F32, name=f"neg_max{c}", tag=f"neg_max{c}", align_bytes=64)
             nc.vector.tensor_scalar(
-                out=flipped[:, c, :],
+                out=flipped[:, c, :N],
                 in0=scores[c][:],
                 scalar1=-1.0,
-                scalar2=sink_n[:, c : c + 1],
+                scalar2=flipped[:, c, N : N + 1],
                 op0=MULT,
                 op1=MIN,
-                accum_out=least[:],
+                accum_out=neg_max[:, c : c + 1],
             )
-            neg_max.append(least)
         v_g1 = keep.tile([P, N], BF16, name="v_g1", tag="q_cast", align_bytes=64)
         nc.vector.tensor_copy(v_g1[:].rearrange("p (u s e) -> p s u e", u=2, e=2), v_raw[1][:].indirect(offs_t[:]))
-        terms = keep.tile([P, 2, 3], F32, name="terms", tag="terms")
+        terms = keep.tile([P, 2, 2], F32, name="terms", tag="terms")
         totals = keep.tile([P, 2], F32, name="totals")
-        passed = keep.tile([P, 3], F32, name="passed")
         p_banks = []
         for c in range(2):
             p_ps = psum.tile([P, 4, P], F32, name=f"p_ps{c}", tag=f"p{c}")
-            dealt = scores[c][:].rearrange("q (t s) -> q t s", t=4)
             for half in range(2):
-                places = slice(2 * half, 2 * half + 2)
-                p = keep.tile([P, 2, P], F32, name=f"p{c}{half}", tag=f"p{c}{half}", align_bytes=64)
+                first = N // 2 * (1 - half)
+                source = (flipped[:, c, N // 2 : N + 1], scores[c][:, : N // 2])[half]
+                p = keep.tile([P, N // 2 + 1 - half], F32, name=f"p{c}{half}", tag=f"p{c}{half}", align_bytes=64)
                 nc.scalar.activation(
                     out=p[:],
-                    in_=dealt[:, places, :],
+                    in_=source,
                     func=EXP,
-                    bias=neg_max[c][:],
-                    scale=1.0,
+                    bias=neg_max[:, c : c + 1],
+                    scale=(-1.0, 1.0)[half],
                     accum_out=terms[:, c, half : half + 1],
                 )
                 for t in range(2):
-                    nc.tensor.transpose(p_ps[:, 2 * half + t, :], p[:, t, :], ident[:])
-                if half == 1:
-                    nc.scalar.activation(
-                        out=terms[:, c, 2:3], in_=sink_n[:, c : c + 1], func=EXP, bias=neg_max[c][:], scale=-1.0
-                    )
-            if c == 1:
-                v_s0 = interleave_values(0, v_ps0)
-                nc.scalar.activation(out=passed[:], in_=terms[:, c, :], func=IDENTITY, accum_out=totals[:, c : c + 1])
-            else:
-                nc.gpsimd.tensor_scalar(
-                    out=totals[:, c : c + 1],
-                    in0=terms[:, c, 0:1],
-                    scalar1=terms[:, c, 1:2],
-                    scalar2=terms[:, c, 2:3],
-                    op0=ADD,
-                    op1=ADD,
-                )
+                    nc.tensor.transpose(p_ps[:, first // P + t, :], p[:, tiles[t]], ident[:])
             p_banks.append(p_ps)
+        nc.gpsimd.tensor_tensor(out=totals[:, 0:1], in0=terms[:, 0, 0:1], in1=terms[:, 0, 1:2], op=ADD)
+        v_s0 = interleave_values(0, v_ps0)
+        nc.scalar.activation(out=totals[:, 1:2], in_=terms[:, 1, 0:1], func=IDENTITY, bias=terms[:, 1, 1:2])
         v_ps1 = turn_values(1, v_g1, "score1")
 
         w_codes = keep.tile([P, NQ], U32, name="w_codes", align_bytes=64)
@@ -240,11 +227,9 @@ def tile_attend_x_router_sink_kernel(tc, xq, kT, vT, vs, sink, offs, qoffs, out)
             recip = keep.tile([P, 1], F32, name=f"recip{c}", tag=("recip0", "w_s0")[c], align_bytes=64)
             if c == 0:
                 nc.gpsimd.tensor_tensor(out=recip[:], in0=totals[:, c : c + 1], in1=minus_one[:], op=POW)
-            else:
-                nc.vector.reciprocal(out=recip[:], in_=totals[:, c : c + 1])
-            if c == 0:
                 r_ps = v_ps1[:, 2, :]
             else:
+                nc.vector.reciprocal(out=recip[:], in_=totals[:, c : c + 1])
                 r_bank = psum.tile([P, P], F32, name="r_bank", tag="row")
                 r_ps = r_bank[:]
             nc.tensor.transpose(r_ps, recip[:].to_broadcast([P, P]), ident[:])

@@ -250,10 +250,13 @@ def tile_attend_x_router_sink_kernel(tc, xq, kT, vT, vs, sink, offs, qoffs, out)
                 start=True,
                 stop=True,
             )
+            return y_ps
+
+        def copy_product(y_ps, tag):
             if tag == "y0":
                 y = v_g1[:].bitcast(F32)[:, :P]
             else:
-                y_tile = keep.tile([P, width], F32, name=f"y_{tag}")
+                y_tile = keep.tile([P, P], F32, name=f"y_{tag}")
                 y = y_tile[:]
             nc.scalar.activation(out=y, in_=y_ps[:], func=COPY)
             return y
@@ -267,14 +270,19 @@ def tile_attend_x_router_sink_kernel(tc, xq, kT, vT, vs, sink, offs, qoffs, out)
         quantise_weights(0, w_s0)
         v_s1 = interleave_values(1, v_ps1)
         copy_reciprocals(0, r_ps0)
-        y_first = multiply(v_mx0, tiles[0], "y0")
+        y_first = copy_product(multiply(v_mx0, tiles[0], "y0"), "y0")
         w_s1 = weigh(1)
         copy_reciprocals(1, spread_reciprocals(1))
         v_mx1 = quantise_values(1, v_s1)
         quantise_weights(1, w_s1)
-        y_second = multiply(v_mx0, tiles[1], "y1")
+        y_second = copy_product(multiply(v_mx0, tiles[1], "y1"), "y1")
+        third_ps = multiply(v_mx1, tiles[0], "score0")
+        y_fourth = copy_product(multiply(v_mx1, tiles[1], "p0"), "p0")
         place(0, y_first, tiles[0], lists[0])
+        y_third = keep.tile([P, P], F32, name="y_third", tag="y_third")
+        nc.vector.tensor_tensor(out=y_third[:], in0=third_ps[:], in1=recip_b[:, tiles[0]], op=MULT)
         place(0, y_second, tiles[1], lists[1])
         nc.sync.dma_start(out=out[tiles[0], :], in_=placed[0][:])
-        place(1, multiply(v_mx1, slice(0, NQ), "score0"), slice(0, NQ), slice(0, NQ // 16))
+        nc.scalar.activation(out=placed[1][:].indirect(qoffs_t[:, lists[0]]), in_=y_third[:], func=COPY)
+        place(1, y_fourth, tiles[1], lists[1])
         nc.sync.dma_start(out=out[tiles[1], :], in_=placed[1][:])

@@ -24,8 +24,8 @@ POW = mybir.AluOpType.pow
 MULT = mybir.AluOpType.mult
 MIN = mybir.AluOpType.min
 
-VECTOR_SLOTS = 128
-SCALAR_TOKENS = 512
+ROW_ALIGN = 256
+VECTOR_SLOTS = 256
 
 
 def tile_attend_x_router_sink_kernel(tc, xq, kT, vT, vs, sink, offs, qoffs, out):
@@ -40,60 +40,61 @@ def tile_attend_x_router_sink_kernel(tc, xq, kT, vT, vs, sink, offs, qoffs, out)
         qoffs_t = keep.tile([P, NQ // 16], U16, name="qoffs_t")
         sink_row = keep.tile([P, NQ], F32, name="sink_row")
         vs_raw = keep.tile([P, T], F32, name="vs_raw")
+        minus_one = keep.tile([P, 1], F32, name="minus_one")
+        one = keep.tile([P, 1], F32, name="one")
+        nc.vector.memset(one[:], 1.0)
+        nc.scalar.activation(out=minus_one[:], in_=one[:], func=COPY, scale=-1.0)
         nc.vector.memset(vs_raw[:LAST, :], 0.0)
         nc.vector.memset(sink_row[:LAST, :], 0.0)
-        k_raw = [keep.tile([P, T], F32, name=f"k_raw{j}") for j in range(4)]
-        v_raw = [keep.tile([P, T], F32, name=f"v_raw{h}", tag=f"v_raw{h}", align_bytes=64) for h in range(2)]
-        q_raw = [keep.tile([P, T], F32, name=f"q_raw{j}") for j in range(4)]
-        k_rows = kT.rearrange("(p j) n -> p j n", j=4)
+        k_raw = [keep.tile([P, 2 * T], F32, name=f"k_raw{g}", align_bytes=ROW_ALIGN) for g in range(2)]
+        q_raw = [keep.tile([P, T], F32, name=f"q_raw{j}", align_bytes=ROW_ALIGN) for j in range(4)]
+        v_raw = [keep.tile([P, T], F32, name=f"v_raw{h}", tag=f"v_raw{h}", align_bytes=ROW_ALIGN) for h in range(2)]
+        k_rows = kT.rearrange("(p g j) n -> p g (j n)", g=2, j=2)
         q_rows = xq.rearrange("(p j) n -> p j n", j=4)
         nc.scalar.dma_start(out=vs_raw[LAST:, :], in_=vs[0:1, :])
         nc.scalar.dma_start(out=sink_row[LAST:, :], in_=sink.rearrange("b q o -> b (q o)"))
         nc.sync.dma_start(out=k_raw[0][:], in_=k_rows[:, 0, :])
         nc.sync.dma_start(offs_t[:], offs)
-        for j in range(1, 3):
-            nc.sync.dma_start(out=k_raw[j][:], in_=k_rows[:, j, :])
+        nc.sync.dma_start(out=k_raw[1][:], in_=k_rows[:, 1, :])
         nc.sync.dma_start(qoffs_t[:], qoffs)
-        nc.sync.dma_start(out=k_raw[3][:], in_=k_rows[:, 3, :])
-        for j in range(4):
+        for j in (0, 2, 1, 3):
             nc.sync.dma_start(out=q_raw[j][:], in_=q_rows[:, j, :])
         for h in range(2):
             nc.sync.dma_start(out=v_raw[h][:], in_=vT[tiles[h], :])
 
         ident = keep.tile([P, P], F32, name="ident")
         make_identity(nc, ident[:])
-        minus_one = keep.tile([P, 1], F32, name="minus_one")
-        nc.gpsimd.memset(minus_one[:], -1.0)
-        placed = [keep.tile([P, T], F32, name=f"placed{h}") for h in range(2)]
+        placed = [keep.tile([P, T], F32, name=f"placed{h}", align_bytes=ROW_ALIGN) for h in range(2)]
         for h in range(2):
             nc.gpsimd.memset(placed[h][:], 0.0)
 
+        def gather_on_vector(dst, window, entries):
+            nc.vector.tensor_copy(dst, window.indirect(entries))
+
+        def gather_on_scalar(dst, window, entries):
+            nc.scalar.activation(out=dst, in_=window.indirect(entries), func=COPY)
+
+        sink_ps = psum.tile([P, 2, P], F32, name="sink_ps", tag="row")
+        for c in range(2):
+            nc.tensor.transpose(sink_ps[:, c, :], sink_row[:, tiles[c]], ident[:])
         vs_g = keep.tile([P, N], F32, name="vs_g")
         nc.vector.tensor_copy(vs_g[:], vs_raw[:].indirect(offs_t[:]))
         vs_ps = psum.tile([P, 4, P], F32, name="vs_ps", tag="value")
         for t in range(4):
             nc.tensor.transpose(vs_ps[:, t, :], vs_g[:, t::4], ident[:])
-        sink_ps = psum.tile([P, 2, P], F32, name="sink_ps", tag="row")
-        for c in range(2):
-            nc.tensor.transpose(sink_ps[:, c, :], sink_row[:, tiles[c]], ident[:])
 
         k_g = keep.tile([P, N * 4], BF16, name="k_g", align_bytes=64)
         flipped = keep.tile([P, 2, N + 16], F32, name="flipped", align_bytes=64)
         sink_n = flipped[:, :, N]
+        nc.scalar.activation(out=sink_n, in_=sink_ps[:, :, LAST], func=COPY, scale=-1.0)
         vs_c = [keep.tile([P, 4], F32, name=f"vs_c{c}", tag=f"vs_c{c}", align_bytes=64) for c in range(2)]
         for c in range(2):
             nc.scalar.activation(out=vs_c[c][:], in_=vs_ps[:, :, LAST], func=COPY)
-        nc.scalar.activation(out=sink_n, in_=sink_ps[:, :, LAST], func=COPY, scale=-1.0)
-        k_planes = keep.tile([P, 2, N], BF16, name="k_planes")
         k_pairs = keep.tile([P, 4 * N], BF16, name="k_pairs")
-        pair_places = k_pairs[:].rearrange("p (u t s e) -> p u s t e", u=2, t=4, e=2)
-        k_cast = keep.tile([P, T], BF16, name="k_cast")
-        nc.scalar.activation(out=k_cast[:], in_=k_raw[0][:], func=COPY)
-        nc.scalar.activation(out=k_planes[:, 0, :], in_=k_cast[:].indirect(offs_t[:]), func=COPY)
-        nc.vector.tensor_copy(k_planes[:, 1, :], k_raw[1][:].indirect(offs_t[:]))
-        nc.scalar.copy(out=pair_places[:, 0], in_=k_planes[:].rearrange("p e (s t) -> p s t e", t=4))
-        for e in range(2):
-            nc.vector.tensor_copy(pair_places[:, 1, :, :, e], k_raw[2 + e][:].indirect(offs_t[:]))
+        pair_places = k_pairs[:].rearrange("p (u t s e) -> p u e s t", u=2, t=4, e=2)
+        for g in range(2):
+            gather_on_scalar(pair_places[:, 0, g], k_raw[g][:], offs_t[:])
+            gather_on_vector(pair_places[:, 1, g], k_raw[g][:, T:], offs_t[:])
         nc.vector.tensor_copy(
             out=k_g[:].bitcast(F32).rearrange("p (n u) -> p n u", u=2),
             in_=k_pairs[:].bitcast(F32).rearrange("p (u n) -> p n u", u=2),
@@ -102,16 +103,12 @@ def tile_attend_x_router_sink_kernel(tc, xq, kT, vT, vs, sink, offs, qoffs, out)
         k_scales = keep.tile([P, N], U8, name="k_scales", align_bytes=64)
         nc.vector.quantize_mx(out=k_codes[:].bitcast(FP8X4), scales=k_scales[:], in_=k_g[:])
 
-        q_cast = keep.tile([P, 2, T], BF16, name="q_cast", tag="q_cast", align_bytes=64)
         q_g = keep.tile([P, NQ, 4], BF16, name="q_g", tag="q_g", align_bytes=64)
-        for j in range(2):
-            nc.scalar.activation(out=q_cast[:, j, :], in_=q_raw[j][:], func=COPY)
-        for c in range(2):
-            for j in range(2):
-                nc.scalar.activation(out=q_g[:, tiles[c], j], in_=q_cast[:, j, :].indirect(qoffs_t[:, lists[c]]), func=COPY)
-        nc.vector.tensor_copy(q_g[:, :, 2], q_raw[2][:].indirect(qoffs_t[:]))
-        for c in range(2):
-            nc.vector.tensor_copy(q_g[:, tiles[c], 3], q_raw[3][:].indirect(qoffs_t[:, lists[c]]))
+        for g in range(2):
+            gather_on_scalar(q_g[:, :, g], q_raw[2 * g][:], qoffs_t[:])
+        for g in range(2):
+            gather_on_vector(q_g[:, tiles[0], 2 + g], q_raw[2 * g + 1][:], qoffs_t[:, lists[0]])
+            gather_on_scalar(q_g[:, tiles[1], 2 + g], q_raw[2 * g + 1][:], qoffs_t[:, lists[1]])
         q_codes = keep.tile([P, NQ], U32, name="q_codes", align_bytes=64)
         q_scales = keep.tile([P, NQ], U8, name="q_scales", align_bytes=64)
         for cols in tiles:
@@ -133,7 +130,7 @@ def tile_attend_x_router_sink_kernel(tc, xq, kT, vT, vs, sink, offs, qoffs, out)
             )
             scores.append(score)
 
-        v_g0 = keep.tile([P, N], BF16, name="v_g0", tag="q_g", align_bytes=64)
+        v_g0 = keep.tile([P, N], BF16, name="v_g0", align_bytes=64)
 
         def turn_values(h, v_g, tag):
             words = v_g[:].bitcast(F32)
@@ -155,17 +152,12 @@ def tile_attend_x_router_sink_kernel(tc, xq, kT, vT, vs, sink, offs, qoffs, out)
             nc.vector.quantize_mx(out=codes[:].bitcast(FP8X4), scales=scales[:], in_=v_s[:])
             return codes, scales
 
-        v_cast = keep.tile([P, T], BF16, name="v_cast", tag="q_cast", align_bytes=64)
-        nc.scalar.activation(out=v_cast[:, :SCALAR_TOKENS], in_=v_raw[0][:, :SCALAR_TOKENS], func=COPY)
-        nc.vector.tensor_copy(out=v_cast[:, SCALAR_TOKENS:], in_=v_raw[0][:, SCALAR_TOKENS:])
         v0_places = v_g0[:].rearrange("p (u s e) -> p s u e", u=2, e=2)
-        nc.vector.tensor_copy(v0_places[:, : VECTOR_SLOTS // 4], v_raw[0][:].indirect(offs_t[:, : VECTOR_SLOTS // 16]))
-        nc.scalar.activation(
-            out=v0_places[:, VECTOR_SLOTS // 4 :], in_=v_cast[:].indirect(offs_t[:, VECTOR_SLOTS // 16 :]), func=COPY
-        )
+        gather_on_vector(v0_places[:, : VECTOR_SLOTS // 4], v_raw[0][:], offs_t[:, : VECTOR_SLOTS // 16])
+        gather_on_scalar(v0_places[:, VECTOR_SLOTS // 4 :], v_raw[0][:], offs_t[:, VECTOR_SLOTS // 16 :])
         v_ps0 = turn_values(0, v_g0, "value")
 
-        neg_max = keep.tile([P, 2], F32, name="neg_max", tag="v_raw0", align_bytes=64)
+        neg_max = keep.tile([P, 2], F32, name="neg_max", tag="v_raw0", align_bytes=ROW_ALIGN)
         for c in range(2):
             nc.vector.tensor_scalar(
                 out=flipped[:, c, :N],
@@ -176,7 +168,7 @@ def tile_attend_x_router_sink_kernel(tc, xq, kT, vT, vs, sink, offs, qoffs, out)
                 op1=MIN,
                 accum_out=neg_max[:, c : c + 1],
             )
-        v_g1 = keep.tile([P, N], BF16, name="v_g1", tag="q_cast", align_bytes=64)
+        v_g1 = keep.tile([P, N], BF16, name="v_g1", align_bytes=64)
         nc.vector.tensor_copy(v_g1[:].rearrange("p (u s e) -> p s u e", u=2, e=2), v_raw[1][:].indirect(offs_t[:]))
         terms = keep.tile([P, 2, 2], F32, name="terms", tag="terms")
         totals = keep.tile([P, 2], F32, name="totals")

@@ -25,7 +25,6 @@ MULT = mybir.AluOpType.mult
 MIN = mybir.AluOpType.min
 
 ROW_ALIGN = 256
-VECTOR_SLOTS = 256
 
 
 def tile_attend_x_router_sink_kernel(tc, xq, kT, vT, vs, sink, offs, qoffs, out):
@@ -59,8 +58,9 @@ def tile_attend_x_router_sink_kernel(tc, xq, kT, vT, vs, sink, offs, qoffs, out)
         nc.sync.dma_start(qoffs_t[:], qoffs)
         for j in (0, 2, 1, 3):
             nc.sync.dma_start(out=q_raw[j][:], in_=q_rows[:, j, :])
-        for h in range(2):
-            nc.sync.dma_start(out=v_raw[h][:], in_=vT[tiles[h], :])
+        nc.sync.dma_start(out=v_raw[0][:], in_=vT[tiles[0], :])
+        for cols in (slice(0, 384), slice(384, 704), slice(704, T)):
+            nc.sync.dma_start(out=v_raw[1][:, cols], in_=vT[tiles[1], cols])
 
         ident = keep.tile([P, P], F32, name="ident")
         make_identity(nc, ident[:])
@@ -153,11 +153,10 @@ def tile_attend_x_router_sink_kernel(tc, xq, kT, vT, vs, sink, offs, qoffs, out)
             return codes, scales
 
         v0_places = v_g0[:].rearrange("p (u s e) -> p s u e", u=2, e=2)
-        gather_on_vector(v0_places[:, : VECTOR_SLOTS // 4], v_raw[0][:], offs_t[:, : VECTOR_SLOTS // 16])
-        gather_on_scalar(v0_places[:, VECTOR_SLOTS // 4 :], v_raw[0][:], offs_t[:, VECTOR_SLOTS // 16 :])
+        gather_on_scalar(v0_places, v_raw[0][:], offs_t[:])
         v_ps0 = turn_values(0, v_g0, "value")
 
-        neg_max = keep.tile([P, 2], F32, name="neg_max", tag="v_raw0", align_bytes=ROW_ALIGN)
+        neg_max = keep.tile([P, 2], F32, name="neg_max")
         for c in range(2):
             nc.vector.tensor_scalar(
                 out=flipped[:, c, :N],

@@ -42,26 +42,31 @@ def tile_attend_x_router_sink_kernel(tc, xq, kT, vT, vs, sink, offs, qoffs, out)
         minus_one = keep.tile([P, 1], F32, name="minus_one")
         one = keep.tile([P, 1], F32, name="one")
         nc.vector.memset(one[:], 1.0)
-        nc.scalar.activation(out=minus_one[:], in_=one[:], func=COPY, scale=-1.0)
         nc.vector.memset(vs_raw[:LAST, :], 0.0)
         nc.vector.memset(sink_row[:LAST, :], 0.0)
         k_raw = [keep.tile([P, 2 * T], F32, name=f"k_raw{g}", align_bytes=ROW_ALIGN) for g in range(2)]
-        q_raw = [keep.tile([P, T], F32, name=f"q_raw{j}", align_bytes=ROW_ALIGN) for j in range(4)]
+        q_first = keep.tile([P, 2 * T], F32, name="q_first", align_bytes=ROW_ALIGN)
+        q_raw = [keep.tile([P, T], F32, name=f"q_raw{j}", align_bytes=ROW_ALIGN) for j in range(2)]
         v_raw = [keep.tile([P, T], F32, name=f"v_raw{h}", tag=f"v_raw{h}", align_bytes=ROW_ALIGN) for h in range(2)]
         k_rows = kT.rearrange("(p g j) n -> p g (j n)", g=2, j=2)
-        q_rows = xq.rearrange("(p j) n -> p j n", j=4)
-        nc.scalar.dma_start(out=vs_raw[LAST:, :], in_=vs[0:1, :])
-        nc.scalar.dma_start(out=sink_row[LAST:, :], in_=sink.rearrange("b q o -> b (q o)"))
+        q_rows = xq.rearrange("(p j) n -> p (j n)", j=4)
+        halves = (slice(0, T // 2), slice(T // 2, T))
+        for half in halves:
+            nc.scalar.dma_start(out=vs_raw[LAST:, half], in_=vs[0:1, half])
+        for cols in tiles:
+            nc.scalar.dma_start(out=sink_row[LAST:, cols], in_=sink.rearrange("b q o -> b (q o)")[:, cols])
         nc.sync.dma_start(out=k_raw[0][:], in_=k_rows[:, 0, :])
         nc.sync.dma_start(offs_t[:], offs)
         nc.sync.dma_start(out=k_raw[1][:], in_=k_rows[:, 1, :])
         nc.sync.dma_start(qoffs_t[:], qoffs)
-        for j in (0, 2, 1, 3):
-            nc.sync.dma_start(out=q_raw[j][:], in_=q_rows[:, j, :])
+        nc.sync.dma_start(out=q_first[:], in_=q_rows[:, : 2 * T])
+        for j in (1, 0):
+            nc.sync.dma_start(out=q_raw[j][:], in_=q_rows[:, (2 + j) * T : (3 + j) * T])
         nc.sync.dma_start(out=v_raw[0][:], in_=vT[tiles[0], :])
-        for cols in (slice(0, 384), slice(384, 704), slice(704, T)):
-            nc.sync.dma_start(out=v_raw[1][:, cols], in_=vT[tiles[1], cols])
+        for half in halves:
+            nc.sync.dma_start(out=v_raw[1][:, half], in_=vT[tiles[1], half])
 
+        nc.scalar.activation(out=minus_one[:], in_=one[:], func=COPY, scale=-1.0)
         ident = keep.tile([P, P], F32, name="ident")
         make_identity(nc, ident[:])
         placed = [keep.tile([P, T], F32, name=f"placed{h}", align_bytes=ROW_ALIGN) for h in range(2)]
@@ -78,7 +83,8 @@ def tile_attend_x_router_sink_kernel(tc, xq, kT, vT, vs, sink, offs, qoffs, out)
         for c in range(2):
             nc.tensor.transpose(sink_ps[:, c, :], sink_row[:, tiles[c]], ident[:])
         vs_g = keep.tile([P, N], F32, name="vs_g")
-        nc.vector.tensor_copy(vs_g[:], vs_raw[:].indirect(offs_t[:]))
+        gather_on_scalar(vs_g[:, : N // 2], vs_raw[:], offs_t[:, : N // 32])
+        gather_on_vector(vs_g[:, N // 2 :], vs_raw[:], offs_t[:, N // 32 :])
         vs_ps = psum.tile([P, 4, P], F32, name="vs_ps", tag="value")
         for t in range(4):
             nc.tensor.transpose(vs_ps[:, t, :], vs_g[:, t::4], ident[:])
@@ -104,11 +110,11 @@ def tile_attend_x_router_sink_kernel(tc, xq, kT, vT, vs, sink, offs, qoffs, out)
         nc.vector.quantize_mx(out=k_codes[:].bitcast(FP8X4), scales=k_scales[:], in_=k_g[:])
 
         q_g = keep.tile([P, NQ, 4], BF16, name="q_g", tag="q_g", align_bytes=64)
-        for g in range(2):
-            gather_on_scalar(q_g[:, :, g], q_raw[2 * g][:], qoffs_t[:])
-        for g in range(2):
-            gather_on_vector(q_g[:, tiles[0], 2 + g], q_raw[2 * g + 1][:], qoffs_t[:, lists[0]])
-            gather_on_scalar(q_g[:, tiles[1], 2 + g], q_raw[2 * g + 1][:], qoffs_t[:, lists[1]])
+        gather_on_scalar(q_g[:, :, 0], q_first[:], qoffs_t[:])
+        gather_on_vector(q_g[:, :, 2], q_first[:, T:], qoffs_t[:])
+        gather_on_vector(q_g[:, :, 3], q_raw[1][:], qoffs_t[:])
+        for c in range(2):
+            gather_on_scalar(q_g[:, tiles[c], 1], q_raw[0][:], qoffs_t[:, lists[c]])
         q_codes = keep.tile([P, NQ], U32, name="q_codes", align_bytes=64)
         q_scales = keep.tile([P, NQ], U8, name="q_scales", align_bytes=64)
         for cols in tiles:

@@ -142,7 +142,7 @@ def tile_attend_x_router_sink_kernel(tc, xq, kT, vT, vs, sink, offs, qoffs, out)
             words = v_g[:].bitcast(F32)
             v_ps = psum.tile([P, 3, P], F32, name=f"v_ps{h}", tag=tag)
             for u in range(2):
-                nc.tensor.transpose(v_ps[:, u, :], words[:, tiles[u]], ident[:])
+                nc.tensor.transpose(v_ps[:, u, :], (words[:, tiles[u]], words[:, u::2])[h], ident[:])
             return v_ps
 
         second_values = keep.tile([P, N // 2], F32, name="second_values", align_bytes=64)
@@ -174,7 +174,7 @@ def tile_attend_x_router_sink_kernel(tc, xq, kT, vT, vs, sink, offs, qoffs, out)
                 accum_out=neg_max[:, c : c + 1],
             )
         v_g1 = keep.tile([P, N], BF16, name="v_g1", align_bytes=64)
-        nc.vector.tensor_copy(v_g1[:].rearrange("p (u s e) -> p s u e", u=2, e=2), v_raw[1][:].indirect(offs_t[:]))
+        gather_on_vector(v_g1[:], v_raw[1][:], offs_t[:])
         terms = keep.tile([P, 2, 2], F32, name="terms", tag="terms")
         totals = keep.tile([P, 2], F32, name="totals")
         p_banks = []

from contextlib import ExitStack

import concourse.mybir as mybir
from concourse.masks import make_identity

D, T, N, NQ, DV = 512, 1024, 512, 256, 256
P = 128
LAST = P - 1
FLOPS = 2 * NQ * N * D + 2 * NQ * N * DV
BYTES = 4 * (2 * D * T + 2 * DV * T + T + NQ) + 2 * P * (N + NQ) // 16

F32 = mybir.dt.float32
BF16 = mybir.dt.bfloat16
U32 = mybir.dt.uint32
U16 = mybir.dt.uint16
U8 = mybir.dt.uint8
FP8X4 = mybir.dt.float8_e4m3fn_x4

COPY = mybir.ActivationFunctionType.Copy
EXP = mybir.ActivationFunctionType.Exp
IDENTITY = mybir.ActivationFunctionType.Identity
ADD = mybir.AluOpType.add
POW = mybir.AluOpType.pow
MULT = mybir.AluOpType.mult
MIN = mybir.AluOpType.min

ROW_ALIGN = 256


def tile_attend_x_router_sink_kernel(tc, xq, kT, vT, vs, sink, offs, qoffs, out):
    nc = tc.nc
    with ExitStack() as ctx:
        keep = ctx.enter_context(tc.tile_pool(name="keep", bufs=1))
        psum = ctx.enter_context(tc.psum_pool(name="psum", bufs=1))
        tiles = [slice(c * P, (c + 1) * P) for c in range(2)]
        lists = [slice(c * 8, (c + 1) * 8) for c in range(2)]

        offs_t = keep.tile([P, N // 16], U16, name="offs_t")
        qoffs_t = keep.tile([P, NQ // 16], U16, name="qoffs_t")
        sink_row = keep.tile([P, NQ], F32, name="sink_row")
        vs_raw = keep.tile([P, T], F32, name="vs_raw")
        minus_one = keep.tile([P, 1], F32, name="minus_one")
        one = keep.tile([P, 1], F32, name="one")
        nc.vector.memset(one[:], 1.0)
        nc.vector.memset(vs_raw[:LAST, :], 0.0)
        nc.vector.memset(sink_row[:LAST, :], 0.0)
        k_raw = [keep.tile([P, 2 * T], F32, name=f"k_raw{g}", align_bytes=ROW_ALIGN) for g in range(2)]
        q_first = keep.tile([P, 2 * T], F32, name="q_first", align_bytes=ROW_ALIGN)
        q_raw = [keep.tile([P, T], F32, name=f"q_raw{j}", align_bytes=ROW_ALIGN) for j in range(2)]
        v_raw = [keep.tile([P, T], F32, name=f"v_raw{h}", tag=f"v_raw{h}", align_bytes=ROW_ALIGN) for h in range(2)]
        k_rows = kT.rearrange("(p g j) n -> p g (j n)", g=2, j=2)
        q_rows = xq.rearrange("(p j) n -> p (j n)", j=4)
        halves = (slice(0, T // 2), slice(T // 2, T))
        for half in halves:
            nc.scalar.dma_start(out=vs_raw[LAST:, half], in_=vs[0:1, half])
        for cols in tiles:
            nc.scalar.dma_start(out=sink_row[LAST:, cols], in_=sink.rearrange("b q o -> b (q o)")[:, cols])
        nc.sync.dma_start(out=k_raw[0][:], in_=k_rows[:, 0, :])
        nc.sync.dma_start(offs_t[:], offs)
        nc.sync.dma_start(out=k_raw[1][:], in_=k_rows[:, 1, :])
        nc.sync.dma_start(qoffs_t[:], qoffs)
        nc.sync.dma_start(out=q_first[:], in_=q_rows[:, : 2 * T])
        for j in (1, 0):
            nc.sync.dma_start(out=q_raw[j][:], in_=q_rows[:, (2 + j) * T : (3 + j) * T])
        nc.sync.dma_start(out=v_raw[0][:], in_=vT[tiles[0], :])
        for half in halves:
            nc.sync.dma_start(out=v_raw[1][:, half], in_=vT[tiles[1], half])

        nc.scalar.activation(out=minus_one[:], in_=one[:], func=COPY, scale=-1.0)
        ident = keep.tile([P, P], F32, name="ident")
        make_identity(nc, ident[:])
        placed = [keep.tile([P, T], F32, name=f"placed{h}", align_bytes=ROW_ALIGN) for h in range(2)]
        for h in range(2):
            nc.gpsimd.memset(placed[h][:], 0.0)

        def gather_on_vector(dst, window, entries):
            nc.vector.tensor_copy(dst, window.indirect(entries))

        def gather_on_scalar(dst, window, entries):
            nc.scalar.activation(out=dst, in_=window.indirect(entries), func=COPY)

        sink_ps = psum.tile([P, 2, P], F32, name="sink_ps", tag="row")
        for c in range(2):
            nc.tensor.transpose(sink_ps[:, c, :], sink_row[:, tiles[c]], ident[:])
        vs_g = keep.tile([P, N], F32, name="vs_g")
        gather_on_scalar(vs_g[:, : N // 2], vs_raw[:], offs_t[:, : N // 32])
        gather_on_vector(vs_g[:, N // 2 :], vs_raw[:], offs_t[:, N // 32 :])
        vs_ps = psum.tile([P, 4, P], F32, name="vs_ps", tag="value")
        for t in range(4):
            nc.tensor.transpose(vs_ps[:, t, :], vs_g[:, t::4], ident[:])

        k_g = keep.tile([P, N * 4], BF16, name="k_g", align_bytes=64)
        flipped = keep.tile([P, 2, N + 16], F32, name="flipped", align_bytes=64)
        sink_n = flipped[:, :, N]
        nc.scalar.activation(out=sink_n, in_=sink_ps[:, :, LAST], func=COPY, scale=-1.0)
        vs_c = [keep.tile([P, 4], F32, name=f"vs_c{c}", tag=f"vs_c{c}", align_bytes=64) for c in range(2)]
        for c in range(2):
            nc.scalar.activation(out=vs_c[c][:], in_=vs_ps[:, :, LAST], func=COPY)
        k_pairs = keep.tile([P, 4 * N], BF16, name="k_pairs")
        pair_places = k_pairs[:].rearrange("p (u t s e) -> p u e s t", u=2, t=4, e=2)
        for g in range(2):
            gather_on_scalar(pair_places[:, 0, g], k_raw[g][:], offs_t[:])
            gather_on_vector(pair_places[:, 1, g], k_raw[g][:, T:], offs_t[:])
        nc.vector.tensor_copy(
            out=k_g[:].bitcast(F32).rearrange("p (n u) -> p n u", u=2),
            in_=k_pairs[:].bitcast(F32).rearrange("p (u n) -> p n u", u=2),
        )
        k_codes = keep.tile([P, N], U32, name="k_codes", align_bytes=64)
        k_scales = keep.tile([P, N], U8, name="k_scales", align_bytes=64)
        nc.vector.quantize_mx(out=k_codes[:].bitcast(FP8X4), scales=k_scales[:], in_=k_g[:])

        q_g = keep.tile([P, NQ, 4], BF16, name="q_g", tag="q_g", align_bytes=64)
        gather_on_scalar(q_g[:, :, 0], q_first[:], qoffs_t[:])
        gather_on_vector(q_g[:, :, 2], q_first[:, T:], qoffs_t[:])
        gather_on_vector(q_g[:, :, 3], q_raw[1][:], qoffs_t[:])
        for c in range(2):
            gather_on_scalar(q_g[:, tiles[c], 1], q_raw[0][:], qoffs_t[:, lists[c]])
        q_codes = keep.tile([P, NQ], U32, name="q_codes", align_bytes=64)
        q_scales = keep.tile([P, NQ], U8, name="q_scales", align_bytes=64)
        for cols in tiles:
            nc.vector.quantize_mx(
                out=q_codes[:, cols].bitcast(FP8X4), scales=q_scales[:, cols], in_=q_g[:, cols, :].rearrange("p q j -> p (q j)")
            )

        scores = []
        for c in range(2):
            score = psum.tile([P, N], F32, name=f"score{c}", tag=f"score{c}")
            nc.tensor.matmul_mx(
                out=score[:],
                lhsT=q_codes[:, tiles[c]].bitcast(FP8X4),
                lhsT_scale=q_scales[:, tiles[c]],
                rhs=k_codes[:].bitcast(FP8X4),
                rhs_scale=k_scales[:],
                start=True,
                stop=True,
            )
            scores.append(score)

        v_g0 = keep.tile([P, N], BF16, name="v_g0", align_bytes=64)

        def turn_values(h, v_g, tag):
            words = v_g[:].bitcast(F32)
            v_ps = psum.tile([P, 3, P], F32, name=f"v_ps{h}", tag=tag)
            for u in range(2):
                nc.tensor.transpose(v_ps[:, u, :], (words[:, tiles[u]], words[:, u::2])[h], ident[:])
            return v_ps

        second_values = keep.tile([P, N // 2], F32, name="second_values", align_bytes=64)

        def interleave_values(h, v_ps):
            words = (flipped[:, 1, N // 2 : N], second_values[:])[h]
            nc.scalar.copy(out=words.rearrange("s (e u) -> s e u", u=2), in_=v_ps[:, :2, :].rearrange("s u e -> s e u"))
            return words.bitcast(BF16)

        def quantise_values(h, v_s):
            codes = keep.tile([P, P], U32, name=f"v_codes{h}", tag=("v_codes0", "p11")[h], align_bytes=64)
            scales = keep.tile([P, P], U8, name=f"v_scales{h}", align_bytes=64)
            nc.vector.quantize_mx(out=codes[:].bitcast(FP8X4), scales=scales[:], in_=v_s[:])
            return codes, scales

        v0_places = v_g0[:].rearrange("p (u s e) -> p s u e", u=2, e=2)
        gather_on_scalar(v0_places, v_raw[0][:], offs_t[:])
        v_ps0 = turn_values(0, v_g0, "value")

        neg_max = keep.tile([P, 2], F32, name="neg_max")
        for c in range(2):
            nc.vector.tensor_scalar(
                out=flipped[:, c, :N],
                in0=scores[c][:],
                scalar1=-1.0,
                scalar2=flipped[:, c, N : N + 1],
                op0=MULT,
                op1=MIN,
                accum_out=neg_max[:, c : c + 1],
            )
        v_g1 = keep.tile([P, N], BF16, name="v_g1", align_bytes=64)
        gather_on_vector(v_g1[:], v_raw[1][:], offs_t[:])
        terms = keep.tile([P, 2, 2], F32, name="terms", tag="terms")
        totals = keep.tile([P, 2], F32, name="totals")
        p_banks = []
        for c in range(2):
            p_ps = psum.tile([P, 4, P], F32, name=f"p_ps{c}", tag=f"p{c}")
            for half in range(2):
                first = N // 2 * (1 - half)
                source = (flipped[:, c, N // 2 : N + 1], scores[c][:, : N // 2])[half]
                p = keep.tile([P, N // 2 + 1 - half], F32, name=f"p{c}{half}", tag=f"p{c}{half}", align_bytes=64)
                nc.scalar.activation(
                    out=p[:],
                    in_=source,
                    func=EXP,
                    bias=neg_max[:, c : c + 1],
                    scale=(-1.0, 1.0)[half],
                    accum_out=terms[:, c, half : half + 1],
                )
                for t in range(2):
                    nc.tensor.transpose(p_ps[:, first // P + t, :], p[:, tiles[t]], ident[:])
            p_banks.append(p_ps)
        nc.gpsimd.tensor_tensor(out=totals[:, 0:1], in0=terms[:, 0, 0:1], in1=terms[:, 0, 1:2], op=ADD)
        v_s0 = interleave_values(0, v_ps0)
        nc.scalar.activation(out=totals[:, 1:2], in_=terms[:, 1, 0:1], func=IDENTITY, bias=terms[:, 1, 1:2])
        v_ps1 = turn_values(1, v_g1, "score1")

        w_codes = keep.tile([P, NQ], U32, name="w_codes", align_bytes=64)
        w_scales = keep.tile([P, NQ], U8, name="w_scales", align_bytes=64)

        def weigh(c):
            w_s = keep.tile([P, P, 4], BF16, name=f"w_s{c}", tag=("w_s0", "vs_c0")[c], align_bytes=64)
            nc.vector.tensor_tensor(
                out=w_s[:],
                in0=p_banks[c][:].rearrange("s t q -> s q t"),
                in1=vs_c[c][:].unsqueeze(1).to_broadcast([P, P, 4]),
                op=MULT,
            )
            return w_s

        def quantise_weights(c, w_s):
            nc.vector.quantize_mx(
                out=w_codes[:, tiles[c]].bitcast(FP8X4), scales=w_scales[:, tiles[c]], in_=w_s[:].rearrange("s q t -> s (q t)")
            )

        recip_b = keep.tile([P, NQ], F32, name="recip_b", tag="terms")

        def spread_reciprocals(c):
            recip = keep.tile([P, 1], F32, name=f"recip{c}", tag=("recip0", "w_s0")[c], align_bytes=64)
            if c == 0:
                nc.gpsimd.tensor_tensor(out=recip[:], in0=totals[:, c : c + 1], in1=minus_one[:], op=POW)
                r_ps = v_ps1[:, 2, :]
            else:
                nc.vector.reciprocal(out=recip[:], in_=totals[:, c : c + 1])
                r_bank = psum.tile([P, P], F32, name="r_bank", tag="row")
                r_ps = r_bank[:]
            nc.tensor.transpose(r_ps, recip[:].to_broadcast([P, P]), ident[:])
            return r_ps

        def copy_reciprocals(c, r_ps):
            nc.scalar.activation(out=recip_b[:, tiles[c]], in_=r_ps, func=COPY)

        def multiply(v_mx, cols, tag):
            width = cols.stop - cols.start
            y_ps = psum.tile([P, width], F32, name=f"y_ps_{tag}", tag=tag)
            nc.tensor.matmul_mx(
                out=y_ps[:],
                lhsT=v_mx[0][:].bitcast(FP8X4),
                lhsT_scale=v_mx[1][:],
                rhs=w_codes[:, cols].bitcast(FP8X4),
                rhs_scale=w_scales[:, cols],
                start=True,
                stop=True,
            )
            return y_ps

        def copy_product(y_ps, tag):
            if tag == "y0":
                y = v_g1[:].bitcast(F32)[:, :P]
            else:
                y_tile = keep.tile([P, P], F32, name=f"y_{tag}")
                y = y_tile[:]
            nc.scalar.activation(out=y, in_=y_ps[:], func=COPY)
            return y

        def place(h, y, cols, entries):
            nc.vector.tensor_tensor(placed[h][:].indirect(qoffs_t[:, entries]), y, recip_b[:, cols], MULT)

        w_s0 = weigh(0)
        r_ps0 = spread_reciprocals(0)
        v_mx0 = quantise_values(0, v_s0)
        quantise_weights(0, w_s0)
        v_s1 = interleave_values(1, v_ps1)
        copy_reciprocals(0, r_ps0)
        y_first = copy_product(multiply(v_mx0, tiles[0], "y0"), "y0")
        w_s1 = weigh(1)
        copy_reciprocals(1, spread_reciprocals(1))
        v_mx1 = quantise_values(1, v_s1)
        quantise_weights(1, w_s1)
        y_second = copy_product(multiply(v_mx0, tiles[1], "y1"), "y1")
        third_ps = multiply(v_mx1, tiles[0], "score0")
        y_fourth = copy_product(multiply(v_mx1, tiles[1], "p0"), "p0")
        place(0, y_first, tiles[0], lists[0])
        y_third = keep.tile([P, P], F32, name="y_third", tag="y_third")
        nc.vector.tensor_tensor(out=y_third[:], in0=third_ps[:], in1=recip_b[:, tiles[0]], op=MULT)
        place(0, y_second, tiles[1], lists[1])
        nc.sync.dma_start(out=out[tiles[0], :], in_=placed[0][:])
        nc.scalar.activation(out=placed[1][:].indirect(qoffs_t[:, lists[0]]), in_=y_third[:], func=COPY)
        place(1, y_fourth, tiles[1], lists[1])
        nc.sync.dma_start(out=out[tiles[1], :], in_=placed[1][:])
